import numpy as np
import ml_dtypes


def mxq(x, axis, fmt="e4m3"):
    dtype, down = {"e4m3": (ml_dtypes.float8_e4m3fn, 7), "e5m2": (ml_dtypes.float8_e5m2, 14)}[fmt]
    v = np.moveaxis(np.asarray(x, np.float32).astype(ml_dtypes.bfloat16).astype(np.float64), axis, -1)
    blocks = v.reshape(v.shape[:-1] + (-1, 32))
    amax = np.abs(blocks).max(-1, keepdims=True)
    byte = np.maximum(np.where(amax > 0, np.frexp(amax)[1] - 1 + 127, 0) - down, 1)
    scale = np.exp2(byte - 127.0)
    codes = (blocks / scale).astype(np.float32).astype(dtype).astype(np.float64)
    return np.moveaxis((codes * scale).reshape(v.shape), -1, axis)


WIDE = False


def mx_kscale(k):
    if not WIDE:
        return np.ones(k)
    levels = np.array([10, -10, 5, -5, 0])
    if k % 512:
        return np.exp2(np.random.permutation(np.resize(levels, k // 32))).repeat(32)
    a = np.empty((k // 512, 16))
    for p in range(k // 512):
        a[p, :8] = np.random.permutation(np.resize(levels, 8))
        for g in range(8):
            far = levels[np.abs(levels - a[p, g]) >= 10]
            a[p, g + 8] = far[np.random.randint(len(far))]
    return np.exp2(a.ravel()).repeat(32)


def f64(x):
    return np.asarray(x).astype(np.float64)


def striped(idx):
    return np.tile(idx.reshape(-1, 16).T, (8, 1)).astype(np.uint16)


def unstriped(offs):
    return offs[:16].T.reshape(-1).astype(np.int64)


E2M1 = np.array([0.0, 0.5, 1.0, 1.5, 2.0, 3.0, 4.0, 6.0, -0.0, -0.5, -1.0, -1.5, -2.0, -3.0, -4.0, -6.0])


def pack_weight(w, fmt):
    k, n = w.shape
    w = f64(np.asarray(w, np.float32).astype(ml_dtypes.bfloat16)).reshape(k // 32, 32, n)
    amax = np.abs(w).max(1)
    if fmt == "e4m3":
        byte = np.frexp(amax)[1] - 1 + 127 - 7
    else:
        mant, ex = np.frexp(amax / 6.0)
        byte = np.where(mant > 0.5, ex, ex - 1) + 127
    byte = np.clip(np.where(amax > 0, byte, 1), 1, 254)
    scaled = (w * np.exp2(127.0 - byte)[:, None, :]).reshape(k, n).astype(np.float32)
    by_word = np.ascontiguousarray(scaled.reshape(k // 512, 128, 4, n).transpose(0, 1, 3, 2))
    if fmt == "e4m3":
        words = by_word.astype(ml_dtypes.float8_e4m3fn).view(np.uint8)
    else:
        c = by_word.astype(ml_dtypes.float4_e2m1fn).view(np.uint8) & 0xF
        words = (c[..., 0::2] | (c[..., 1::2] << 4)).reshape(k // 512, 128, 2 * n)
    return np.ascontiguousarray(words), np.ascontiguousarray(byte.astype(np.uint8).reshape(k // 512, 16, n))


def unpack_weight(words, scales, fmt):
    g, _, n = scales.shape
    words = np.ascontiguousarray(words).reshape(g, 128, n, -1)
    if fmt == "e4m3":
        vals = words.view(ml_dtypes.float8_e4m3fn).astype(np.float64)
    else:
        nib = np.empty((g, 128, n, 4), np.uint8)
        nib[..., 0::2] = words & 0xF
        nib[..., 1::2] = words >> 4
        vals = E2M1[nib]
    vals = vals * np.repeat(np.exp2(scales.astype(np.float64) - 127.0), 8, axis=1)[..., None]
    return vals.transpose(0, 1, 3, 2).reshape(g * 512, n)


def silu(v):
    return v / (1.0 + np.exp(-np.maximum(v, -700.0)))


K, T, E, C, H, N = 1536, 640, 2, 256, 1024, 128


def by_expert(wq, xq):
    return np.concatenate([wq[e].T @ xq[:, e * C:(e + 1) * C] for e in range(E)], axis=1)


def setup_inputs():
    n = np.random.standard_normal
    s = mx_kscale(K)[:, None]
    u = mx_kscale(H)
    w1 = [pack_weight(m, "e2m1") for m in n((E, K, H)) / np.sqrt(K) / s[None] * u[None, None, :]]
    w2 = [pack_weight(m, "e2m1") for m in n((E, H, N)) / np.sqrt(H) / u[None, :, None]]
    return {
        "xT": (n((K, T)) * s).astype(np.float32),
        "w1_words": np.stack([m[0] for m in w1]),
        "w1_scales": np.stack([m[1] for m in w1]),
        "w2_words": np.stack([m[0] for m in w2]),
        "w2_scales": np.stack([m[1] for m in w2]),
        "gate": np.tile(np.random.uniform(0.2, 1.0, E * C), (N, 1)).astype(np.float32),
        "offs": striped(np.random.permutation(T)[:E * C]),
    }


def reference(xT, w1_words, w1_scales, w2_words, w2_scales, gate, offs):
    idx = unstriped(offs)
    w1 = np.stack([unpack_weight(w1_words[e], w1_scales[e], "e2m1") for e in range(E)])
    w2 = np.stack([unpack_weight(w2_words[e], w2_scales[e], "e2m1") for e in range(E)])
    xq = mxq(f64(xT)[:, idx], 0, "e4m3")
    h = silu(by_expert(w1, xq))
    y = by_expert(w2, mxq(h, 0, "e4m3"))
    out = np.zeros((N, T))
    out[:, idx] = f64(gate) * y
    return out

@@ -1,0 +1,243 @@
+from contextlib import ExitStack
+
+import concourse.mybir as mybir
+from concourse.masks import make_identity
+
+F32 = mybir.dt.float32
+BF16 = mybir.dt.bfloat16
+I32 = mybir.dt.int32
+U32 = mybir.dt.uint32
+U16 = mybir.dt.uint16
+U8 = mybir.dt.uint8
+FP8X4 = mybir.dt.float8_e4m3fn_x4
+FP4X4 = mybir.dt.float4_e2m1fn_x4
+COPY = mybir.ActivationFunctionType.Copy
+SILU = mybir.ActivationFunctionType.Silu
+MULT = mybir.AluOpType.mult
+
+P = 128
+K, T, E, C, H, N = 1536, 640, 2, 256, 1024, 128
+KP = K // 512
+HP = H // 512
+LIST_COLS = E * C // 16
+FLOPS = 2 * E * C * (K * H + H * N)
+
+CHUNKS = (
+    (("s", 0, 256), ("v", 256, 384)),
+    (("s", 0, 640),),
+    (("s", 0, 512), ("v", 512, 128)),
+)
+QUANTS = ((0, 512), (512, 128))
+TURN = ("vv", "vv", "sv", "ss")
+
+
+def tile_moe_pln_mlp_silu_kernel(
+    tc, xT, w1_words, w1_scales, w2_words, w2_scales, gate, offs, out
+):
+    nc = tc.nc
+    with ExitStack() as ctx:
+        lists = ctx.enter_context(tc.tile_pool(name="lists", bufs=1))
+        keep = ctx.enter_context(tc.tile_pool(name="keep", bufs=1))
+        psum = ctx.enter_context(tc.psum_pool(name="psum", bufs=1))
+
+        offsets = lists.tile([P, LIST_COLS], U16, name="offsets")
+
+        warm = keep.tile([P, 1], F32, name="warm")
+        nc.vector.memset(warm[:], 0.0)
+        nc.scalar.activation(warm[:], warm[:], SILU)
+
+        w1s = [keep.tile([P, KP * H], U8, name=f"w1s{e}", align_bytes=64) for e in range(E)]
+        w2s = keep.tile([P, E * HP * N], U8, name="w2s", align_bytes=64)
+        for e in range(E):
+            nc.vector.memset(w1s[e][:].bitcast(I32), 0)
+        nc.vector.memset(w2s[:].bitcast(I32), 0)
+        xsc = []
+        for s in range(KP):
+            t = keep.tile([P, T], U8, name=f"xsc{s}", align_bytes=64)
+            nc.vector.memset(t[:].bitcast(I32), 0)
+            xsc.append(t)
+        result = keep.tile([P, T], F32, name="result")
+        nc.vector.memset(result[:], 0.0)
+
+        ident = keep.tile([P, P], F32, name="ident")
+        make_identity(nc, ident[:])
+
+
+        raw = {}
+        w1 = {}
+
+        def load_x(s):
+            raw[s] = keep.tile([P, 4, T], F32, name=f"raw{s}")
+            nc.sync.dma_start(
+                out=raw[s][:], in_=xT[512 * s : 512 * (s + 1), :].rearrange("(p j) w -> p j w", j=4)
+            )
+
+        def load_w1_scales(e):
+            for r in range(4):
+                nc.sync.dma_start(
+                    out=w1s[e][r:P:32, :].bitcast(I32).rearrange("q (s i) -> q s i", s=KP),
+                    in_=w1_scales[e, :, r:16:4, :].bitcast(I32).rearrange("s q i -> q s i"),
+                )
+
+        def load_w1(e, s):
+            t = keep.tile([P, 2 * H], U8, name=f"w1_{e}_{s}", align_bytes=64)
+            nc.sync.dma_start(out=t[:].bitcast(I32), in_=w1_words[e, s].bitcast(I32))
+            w1[e, s] = t
+
+        load_x(0)
+        nc.sync.dma_start(offsets[:], offs)
+        load_x(1)
+        load_x(2)
+        for e in range(E):
+            load_w1_scales(e)
+            if e == 0:
+                load_w1(0, 0)
+                load_w1(1, 0)
+        for s in range(1, KP):
+            for e in range(E):
+                load_w1(e, s)
+        w2 = keep.tile([P, E * HP, 2 * N], U8, name="w2", align_bytes=64)
+        nc.sync.dma_start(
+            out=w2[:].rearrange("p e b -> p (e b)").bitcast(I32).rearrange("p (e b) -> p e b", e=E * HP),
+            in_=w2_words.bitcast(I32).rearrange("e s p b -> p (e s) b"),
+        )
+        for q in range(4):
+            nc.sync.dma_start(
+                out=w2s[32 * q : 32 * q + 4, :].bitcast(I32).rearrange("q (e i) -> q e i", e=E * HP),
+                in_=w2_scales[:, :, 4 * q : 4 * q + 4, :].bitcast(I32).rearrange("e s q i -> q (e s) i"),
+            )
+        gates = keep.tile([P, E * C], F32, name="gates")
+        nc.sync.dma_start(out=gates[:], in_=gate)
+
+        xw = [keep.tile([P, T], U32, name=f"xw{s}", align_bytes=64) for s in range(KP)]
+        gw, gs, acc = {}, {}, {}
+        for st in range(2 * E):
+            for g in range(HP):
+                acc[st, g] = psum.tile([P, 512], F32, name=f"acc{st}_{g}", tag=f"bank{2 * st + g}")
+
+        def quantise_x(s):
+            mixed = keep.tile([P, T, 4], BF16, name=f"xb{s}", align_bytes=64)
+            for eng, c0, w in CHUNKS[s]:
+                src = raw[s][:, :, c0 : c0 + w].rearrange("p j (c i) -> p c j i", i=4)
+                dst = mixed[:, c0 : c0 + w, :].rearrange("p (c i) j -> p c j i", i=4)
+                if eng == "s":
+                    nc.scalar.activation(dst, src, COPY)
+                else:
+                    nc.vector.tensor_copy(dst, src)
+            for c0, w in QUANTS:
+                nc.vector.quantize_mx(
+                    out=xw[s][:, c0 : c0 + w].bitcast(FP8X4),
+                    scales=xsc[s][:, c0 : c0 + w],
+                    in_=mixed[:, c0 : c0 + w, :].rearrange("p w j -> p (w j)"),
+                )
+
+        for e in range(E):
+            for s in range(KP):
+                gw[e, s] = keep.tile([P, C], U32, name=f"gw{e}_{s}", align_bytes=64)
+                gs[e, s] = keep.tile([P, C], U8, name=f"gs{e}_{s}", align_bytes=64)
+
+        def gather(e, s, lo, n):
+            o = (e * C + lo) // 16
+            idx = offsets[:, o : o + n // 16]
+            nc.vector.tensor_copy(gw[e, s][:, lo : lo + n], xw[s][:].indirect(idx))
+            nc.vector.tensor_copy(gs[e, s][:, lo : lo + n], xsc[s][:].indirect(idx))
+
+        def first_layer(e, s, half):
+            st = 2 * e + half
+            cols = slice(half * P, (half + 1) * P)
+            for g in range(HP):
+                wcol = s * H + g * 512
+                nc.tensor.matmul_mx(
+                    out=acc[st, g][:],
+                    lhsT=gw[e, s][:, cols].bitcast(FP8X4),
+                    lhsT_scale=gs[e, s][:, cols],
+                    rhs=w1[e, s][:, g * 1024 : (g + 1) * 1024].bitcast(FP4X4),
+                    rhs_scale=w1s[e][:, wcol : wcol + 512],
+                    start=(s == 0),
+                    stop=(s == KP - 1),
+                )
+
+        tps = {}
+
+        def hidden(st):
+            hs = keep.tile([P, H], BF16, name=f"hs{st}", align_bytes=64)
+            words = hs[:].bitcast(F32)
+            for g in range(HP):
+                nc.scalar.activation(
+                    hs[:, g * 512 : (g + 1) * 512].rearrange("p (u m d) -> p u m d", u=2, d=2),
+                    acc[st, g][:].rearrange("p (m u d) -> p u m d", u=2, d=2),
+                    SILU,
+                )
+            for g in range(HP):
+                tp = psum.tile([P, 512], F32, name=f"tp{st}_{g}", tag=f"bank{2 * st + g}")
+                for u in range(2):
+                    b = 2 * g + u
+                    nc.tensor.transpose(tp[:, u * P : (u + 1) * P], words[:, b * P : (b + 1) * P], ident[:])
+                tps[st, g] = tp
+
+        ys = {}
+
+        def second_layer(st):
+            e = st // 2
+            y = psum.tile([P, 512], F32, name=f"y{st}", tag=f"bank{2 * st}")
+            hb = keep.tile([P, HP, 512], BF16, name=f"hb{st}", align_bytes=64)
+            hw = keep.tile([P, HP, P], U32, name=f"hw{st}", align_bytes=64)
+            hc = keep.tile([P, HP, P], U8, name=f"hc{st}", align_bytes=64)
+            for g in range(HP):
+                dst = hb[:, g, :].bitcast(F32).rearrange("p (r u) -> p r u", u=2)
+                src = tps[st, g][:, 0 : 2 * P].rearrange("p (u r) -> p r u", u=2)
+                if TURN[st][g] == "s":
+                    nc.scalar.copy(dst, src)
+                else:
+                    nc.vector.tensor_copy(dst, src)
+            nc.vector.quantize_mx(
+                out=hw[:].rearrange("p g r -> p (g r)").bitcast(FP8X4),
+                scales=hc[:].rearrange("p g r -> p (g r)"),
+                in_=hb[:].rearrange("p g c -> p (g c)"),
+            )
+            for g in range(HP):
+                row = e * HP + g
+                nc.tensor.matmul_mx(
+                    out=y[:, 0:P],
+                    lhsT=w2[:, row, :].bitcast(FP4X4),
+                    lhsT_scale=w2s[:, row * N : (row + 1) * N],
+                    rhs=hw[:, g, :].bitcast(FP8X4),
+                    rhs_scale=hc[:, g, :],
+                    start=(g == 0),
+                    stop=(g == HP - 1),
+                )
+            yt = keep.tile([P, P], F32, name=f"yt{st}")
+            nc.scalar.copy(yt[:], y[:, 0:P])
+            ys[st] = yt
+
+        def both(e, s):
+            gather(e, s, 0, C)
+            for half in range(2):
+                first_layer(e, s, half)
+
+        def one(e, s, half):
+            gather(e, s, half * P, P)
+            first_layer(e, s, half)
+
+        quantise_x(0)
+        both(0, 0)
+        quantise_x(1)
+        quantise_x(2)
+        one(1, 0, 0)
+        one(1, 0, 1)
+        both(0, 1)
+        one(0, 2, 0)
+        one(1, 1, 0)
+        one(0, 2, 1)
+        one(1, 2, 0)
+        one(1, 1, 1)
+        one(1, 2, 1)
+        for st in range(2 * E):
+            hidden(st)
+            second_layer(st)
+        for st in range(2 * E):
+            nc.vector.tensor_tensor(
+                result[:].indirect(offsets[:, st * 8 : (st + 1) * 8]), ys[st][:], gates[:, st * P : (st + 1) * P], MULT
+            )
+
+        nc.sync.dma_start(out=out, in_=result[:])

@@ -20,15 +20,13 @@ K, T, E, C, H, N = 1536, 640, 2, 256, 1024, 128
 KP = K // 512
 HP = H // 512
 LIST_COLS = E * C // 16
+TILES = E * C // P
 FLOPS = 2 * E * C * (K * H + H * N)
 
-CHUNKS = (
-    (("s", 0, 256), ("v", 256, 384)),
-    (("s", 0, 640),),
-    (("s", 0, 512), ("v", 512, 128)),
-)
+SCALAR_TOKENS = (224, 512, 384)
 QUANTS = ((0, 512), (512, 128))
-TURN = ("vv", "vv", "sv", "ss")
+TURN = ("vv", "vv", "ss", "ss")
+YCOPY = "vsss"
 
 
 def tile_moe_pln_mlp_silu_kernel(
@@ -42,15 +40,16 @@ def tile_moe_pln_mlp_silu_kernel(
 
         offsets = lists.tile([P, LIST_COLS], U16, name="offsets")
 
+        first_scales = keep.tile([P, E * H], U8, name="w1s_first", align_bytes=64)
+        rest_scales = [keep.tile([P, (KP - 1) * H], U8, name=f"w1s_rest{e}", align_bytes=64) for e in range(E)]
+        w2s = keep.tile([P, E * HP * N], U8, name="w2s", align_bytes=64)
+        for plane in [first_scales] + rest_scales + [w2s]:
+            nc.gpsimd.memset(plane[:].bitcast(I32), 0)
+
         warm = keep.tile([P, 1], F32, name="warm")
         nc.vector.memset(warm[:], 0.0)
         nc.scalar.activation(warm[:], warm[:], SILU)
 
-        w1s = [keep.tile([P, KP * H], U8, name=f"w1s{e}", align_bytes=64) for e in range(E)]
-        w2s = keep.tile([P, E * HP * N], U8, name="w2s", align_bytes=64)
-        for e in range(E):
-            nc.vector.memset(w1s[e][:].bitcast(I32), 0)
-        nc.vector.memset(w2s[:].bitcast(I32), 0)
         xsc = []
         for s in range(KP):
             t = keep.tile([P, T], U8, name=f"xsc{s}", align_bytes=64)
@@ -62,7 +61,6 @@ def tile_moe_pln_mlp_silu_kernel(
         ident = keep.tile([P, P], F32, name="ident")
         make_identity(nc, ident[:])
 
-
         raw = {}
         w1 = {}
 
@@ -72,11 +70,11 @@ def tile_moe_pln_mlp_silu_kernel(
                 out=raw[s][:], in_=xT[512 * s : 512 * (s + 1), :].rearrange("(p j) w -> p j w", j=4)
             )
 
-        def load_w1_scales(e):
+        def load_scales(plane, rows):
             for r in range(4):
                 nc.sync.dma_start(
-                    out=w1s[e][r:P:32, :].bitcast(I32).rearrange("q (s i) -> q s i", s=KP),
-                    in_=w1_scales[e, :, r:16:4, :].bitcast(I32).rearrange("s q i -> q s i"),
+                    out=plane[r:P:32, :].bitcast(I32).rearrange("q (s i) -> q s i", s=rows.shape[0]),
+                    in_=rows[:, r:16:4, :].bitcast(I32).rearrange("s q i -> q s i"),
                 )
 
         def load_w1(e, s):
@@ -84,46 +82,49 @@ def tile_moe_pln_mlp_silu_kernel(
             nc.sync.dma_start(out=t[:].bitcast(I32), in_=w1_words[e, s].bitcast(I32))
             w1[e, s] = t
 
+        def w1_scale(e, s, g):
+            if s == 0:
+                return first_scales[:, e * H + g * 512 : e * H + (g + 1) * 512]
+            return rest_scales[e][:, (s - 1) * H + g * 512 : (s - 1) * H + (g + 1) * 512]
+
         load_x(0)
         nc.sync.dma_start(offsets[:], offs)
         load_x(1)
+        load_scales(first_scales, w1_scales[:, 0])
+        for e in range(E):
+            load_w1(e, 0)
         load_x(2)
         for e in range(E):
-            load_w1_scales(e)
-            if e == 0:
-                load_w1(0, 0)
-                load_w1(1, 0)
-        for s in range(1, KP):
-            for e in range(E):
+            load_scales(rest_scales[e], w1_scales[e, 1:KP])
+            for s in range(1, KP):
                 load_w1(e, s)
         w2 = keep.tile([P, E * HP, 2 * N], U8, name="w2", align_bytes=64)
         nc.sync.dma_start(
             out=w2[:].rearrange("p e b -> p (e b)").bitcast(I32).rearrange("p (e b) -> p e b", e=E * HP),
             in_=w2_words.bitcast(I32).rearrange("e s p b -> p (e s) b"),
         )
-        for q in range(4):
-            nc.sync.dma_start(
-                out=w2s[32 * q : 32 * q + 4, :].bitcast(I32).rearrange("q (e i) -> q e i", e=E * HP),
-                in_=w2_scales[:, :, 4 * q : 4 * q + 4, :].bitcast(I32).rearrange("e s q i -> q (e s) i"),
-            )
+        load_scales(w2s, w2_scales.rearrange("e s q i -> (e s) q i"))
         gates = keep.tile([P, E * C], F32, name="gates")
         nc.sync.dma_start(out=gates[:], in_=gate)
 
         xw = [keep.tile([P, T], U32, name=f"xw{s}", align_bytes=64) for s in range(KP)]
         gw, gs, acc = {}, {}, {}
-        for st in range(2 * E):
+        for st in range(TILES):
             for g in range(HP):
                 acc[st, g] = psum.tile([P, 512], F32, name=f"acc{st}_{g}", tag=f"bank{2 * st + g}")
 
+        def round_x(mixed, s, c0, c1, copy):
+            src = raw[s][:, :, c0:c1].rearrange("p j (c i) -> p c j i", i=4)
+            dst = mixed[:, c0:c1, :].rearrange("p (c i) j -> p c j i", i=4)
+            copy(dst, src)
+
+        def scalar_round(dst, src):
+            nc.scalar.activation(dst, src, COPY)
+
         def quantise_x(s):
             mixed = keep.tile([P, T, 4], BF16, name=f"xb{s}", align_bytes=64)
-            for eng, c0, w in CHUNKS[s]:
-                src = raw[s][:, :, c0 : c0 + w].rearrange("p j (c i) -> p c j i", i=4)
-                dst = mixed[:, c0 : c0 + w, :].rearrange("p (c i) j -> p c j i", i=4)
-                if eng == "s":
-                    nc.scalar.activation(dst, src, COPY)
-                else:
-                    nc.vector.tensor_copy(dst, src)
+            round_x(mixed, s, 0, SCALAR_TOKENS[s], scalar_round)
+            round_x(mixed, s, SCALAR_TOKENS[s], T, nc.vector.tensor_copy)
             for c0, w in QUANTS:
                 nc.vector.quantize_mx(
                     out=xw[s][:, c0 : c0 + w].bitcast(FP8X4),
@@ -142,24 +143,30 @@ def tile_moe_pln_mlp_silu_kernel(
             nc.vector.tensor_copy(gw[e, s][:, lo : lo + n], xw[s][:].indirect(idx))
             nc.vector.tensor_copy(gs[e, s][:, lo : lo + n], xsc[s][:].indirect(idx))
 
-        def first_layer(e, s, half):
-            st = 2 * e + half
+        def first_layer(st, s):
+            e, half = divmod(st, 2)
             cols = slice(half * P, (half + 1) * P)
             for g in range(HP):
-                wcol = s * H + g * 512
                 nc.tensor.matmul_mx(
                     out=acc[st, g][:],
                     lhsT=gw[e, s][:, cols].bitcast(FP8X4),
                     lhsT_scale=gs[e, s][:, cols],
                     rhs=w1[e, s][:, g * 1024 : (g + 1) * 1024].bitcast(FP4X4),
-                    rhs_scale=w1s[e][:, wcol : wcol + 512],
+                    rhs_scale=w1_scale(e, s, g),
                     start=(s == 0),
                     stop=(s == KP - 1),
                 )
 
-        tps = {}
+        ys = {}
 
-        def hidden(st):
+        def move(engine, dst, src):
+            if engine == "s":
+                nc.scalar.copy(dst, src)
+            else:
+                nc.vector.tensor_copy(dst, src)
+
+        def second_layer(st):
+            e = st // 2
             hs = keep.tile([P, H], BF16, name=f"hs{st}", align_bytes=64)
             words = hs[:].bitcast(F32)
             for g in range(HP):
@@ -168,74 +175,67 @@ def tile_moe_pln_mlp_silu_kernel(
                     acc[st, g][:].rearrange("p (m u d) -> p u m d", u=2, d=2),
                     SILU,
                 )
+            tps = []
             for g in range(HP):
                 tp = psum.tile([P, 512], F32, name=f"tp{st}_{g}", tag=f"bank{2 * st + g}")
                 for u in range(2):
                     b = 2 * g + u
                     nc.tensor.transpose(tp[:, u * P : (u + 1) * P], words[:, b * P : (b + 1) * P], ident[:])
-                tps[st, g] = tp
-
-        ys = {}
-
-        def second_layer(st):
-            e = st // 2
+                tps.append(tp)
             y = psum.tile([P, 512], F32, name=f"y{st}", tag=f"bank{2 * st}")
-            hb = keep.tile([P, HP, 512], BF16, name=f"hb{st}", align_bytes=64)
-            hw = keep.tile([P, HP, P], U32, name=f"hw{st}", align_bytes=64)
-            hc = keep.tile([P, HP, P], U8, name=f"hc{st}", align_bytes=64)
+            hb = keep.tile([P, HP * 512], BF16, name=f"hb{st}", align_bytes=64)
+            hw = keep.tile([P, HP * P], U32, name=f"hw{st}", align_bytes=64)
+            hc = keep.tile([P, HP * P], U8, name=f"hc{st}", align_bytes=64)
             for g in range(HP):
-                dst = hb[:, g, :].bitcast(F32).rearrange("p (r u) -> p r u", u=2)
-                src = tps[st, g][:, 0 : 2 * P].rearrange("p (u r) -> p r u", u=2)
-                if TURN[st][g] == "s":
-                    nc.scalar.copy(dst, src)
-                else:
-                    nc.vector.tensor_copy(dst, src)
-            nc.vector.quantize_mx(
-                out=hw[:].rearrange("p g r -> p (g r)").bitcast(FP8X4),
-                scales=hc[:].rearrange("p g r -> p (g r)"),
-                in_=hb[:].rearrange("p g c -> p (g c)"),
-            )
-            for g in range(HP):
-                row = e * HP + g
-                nc.tensor.matmul_mx(
-                    out=y[:, 0:P],
-                    lhsT=w2[:, row, :].bitcast(FP4X4),
-                    lhsT_scale=w2s[:, row * N : (row + 1) * N],
-                    rhs=hw[:, g, :].bitcast(FP8X4),
-                    rhs_scale=hc[:, g, :],
-                    start=(g == 0),
-                    stop=(g == HP - 1),
+                dst = hb[:, g * 512 : (g + 1) * 512].bitcast(F32).rearrange("p (r u) -> p r u", u=2)
+                src = tps[g][:, 0 : 2 * P].rearrange("p (u r) -> p r u", u=2)
+                move(TURN[st][g], dst, src)
+            step = 1 if st == TILES - 1 else HP
+            for g0 in range(0, HP, step):
+                nc.vector.quantize_mx(
+                    out=hw[:, g0 * P : (g0 + step) * P].bitcast(FP8X4),
+                    scales=hc[:, g0 * P : (g0 + step) * P],
+                    in_=hb[:, g0 * 512 : (g0 + step) * 512],
                 )
+                for g in range(g0, g0 + step):
+                    row = e * HP + g
+                    nc.tensor.matmul_mx(
+                        out=y[:, 0:P],
+                        lhsT=w2[:, row, :].bitcast(FP4X4),
+                        lhsT_scale=w2s[:, row * N : (row + 1) * N],
+                        rhs=hw[:, g * P : (g + 1) * P].bitcast(FP8X4),
+                        rhs_scale=hc[:, g * P : (g + 1) * P],
+                        start=(g == 0),
+                        stop=(g == HP - 1),
+                    )
             yt = keep.tile([P, P], F32, name=f"yt{st}")
-            nc.scalar.copy(yt[:], y[:, 0:P])
+            move(YCOPY[st], yt[:], y[:, 0:P])
             ys[st] = yt
 
-        def both(e, s):
-            gather(e, s, 0, C)
-            for half in range(2):
-                first_layer(e, s, half)
-
-        def one(e, s, half):
-            gather(e, s, half * P, P)
-            first_layer(e, s, half)
-
-        quantise_x(0)
-        both(0, 0)
-        quantise_x(1)
-        quantise_x(2)
-        one(1, 0, 0)
-        one(1, 0, 1)
-        both(0, 1)
-        one(0, 2, 0)
-        one(1, 1, 0)
-        one(0, 2, 1)
-        one(1, 2, 0)
-        one(1, 1, 1)
-        one(1, 2, 1)
-        for st in range(2 * E):
-            hidden(st)
-            second_layer(st)
-        for st in range(2 * E):
+        for s in range(KP):
+            quantise_x(s)
+        for e in range(E):
+            gather(e, 0, 0, C)
+            first_layer(2 * e, 0)
+            first_layer(2 * e + 1, 0)
+        gather(0, 1, 0, C)
+        first_layer(0, 1)
+        first_layer(1, 1)
+        for half in range(2):
+            gather(0, 2, half * P, P)
+            first_layer(half, 2)
+        gather(1, 1, 0, C)
+        first_layer(2, 1)
+        first_layer(3, 1)
+        for half in range(2):
+            gather(1, 2, half * P, P)
+        second_layer(0)
+        first_layer(2, 2)
+        second_layer(1)
+        first_layer(3, 2)
+        second_layer(2)
+        second_layer(3)
+        for st in range(TILES):
             nc.vector.tensor_tensor(
                 result[:].indirect(offsets[:, st * 8 : (st + 1) * 8]), ys[st][:], gates[:, st * P : (st + 1) * P], MULT
             )

@@ -23,10 +23,12 @@ LIST_COLS = E * C // 16
 TILES = E * C // P
 FLOPS = 2 * E * C * (K * H + H * N)
 
-SCALAR_TOKENS = (224, 512, 384)
+SCALAR_TOKENS = (256, 512, 448)
 QUANTS = ((0, 512), (512, 128))
 TURN = ("vv", "vv", "ss", "ss")
 YCOPY = "vsss"
+WIDE = 704
+SPLIT = (2, 3,)
 
 
 def tile_moe_pln_mlp_silu_kernel(
@@ -40,11 +42,11 @@ def tile_moe_pln_mlp_silu_kernel(
 
         offsets = lists.tile([P, LIST_COLS], U16, name="offsets")
 
-        first_scales = keep.tile([P, E * H], U8, name="w1s_first", align_bytes=64)
-        rest_scales = [keep.tile([P, (KP - 1) * H], U8, name=f"w1s_rest{e}", align_bytes=64) for e in range(E)]
+        w1s = [keep.tile([P, E * H], U8, name=f"w1s{s}", align_bytes=64) for s in range(KP)]
         w2s = keep.tile([P, E * HP * N], U8, name="w2s", align_bytes=64)
-        for plane in [first_scales] + rest_scales + [w2s]:
-            nc.gpsimd.memset(plane[:].bitcast(I32), 0)
+        nc.gpsimd.memset(w1s[0][:].bitcast(I32), 0)
+        for plane in w1s[1:] + [w2s]:
+            nc.vector.memset(plane[:].bitcast(I32), 0)
 
         warm = keep.tile([P, 1], F32, name="warm")
         nc.vector.memset(warm[:], 0.0)
@@ -52,9 +54,12 @@ def tile_moe_pln_mlp_silu_kernel(
 
         xsc = []
         for s in range(KP):
-            t = keep.tile([P, T], U8, name=f"xsc{s}", align_bytes=64)
+            t = keep.tile([P, WIDE], U8, name=f"xsc{s}", align_bytes=64)
             nc.vector.memset(t[:].bitcast(I32), 0)
             xsc.append(t)
+        xw = [keep.tile([P, WIDE], U32, name=f"xw{s}", align_bytes=64) for s in range(KP)]
+        for s in range(KP):
+            nc.vector.memset(xw[s][:, T:WIDE].bitcast(I32), 0)
         result = keep.tile([P, T], F32, name="result")
         nc.vector.memset(result[:], 0.0)
 
@@ -82,32 +87,35 @@ def tile_moe_pln_mlp_silu_kernel(
             nc.sync.dma_start(out=t[:].bitcast(I32), in_=w1_words[e, s].bitcast(I32))
             w1[e, s] = t
 
+        w2 = keep.tile([P, E * HP, 2 * N], U8, name="w2", align_bytes=64)
+
+        def load_w2():
+            nc.sync.dma_start(
+                out=w2[:].rearrange("p e b -> p (e b)").bitcast(I32).rearrange("p (e b) -> p e b", e=E * HP),
+                in_=w2_words.bitcast(I32).rearrange("e s p b -> p (e s) b"),
+            )
+            load_scales(w2s, w2_scales.rearrange("e s q i -> (e s) q i"))
+
         def w1_scale(e, s, g):
-            if s == 0:
-                return first_scales[:, e * H + g * 512 : e * H + (g + 1) * 512]
-            return rest_scales[e][:, (s - 1) * H + g * 512 : (s - 1) * H + (g + 1) * 512]
+            return w1s[s][:, e * H + g * 512 : e * H + (g + 1) * 512]
 
         load_x(0)
         nc.sync.dma_start(offsets[:], offs)
         load_x(1)
-        load_scales(first_scales, w1_scales[:, 0])
-        for e in range(E):
-            load_w1(e, 0)
+        load_scales(w1s[0], w1_scales[:, 0])
+        load_w1(0, 0)
+        load_w1(1, 0)
         load_x(2)
-        for e in range(E):
-            load_scales(rest_scales[e], w1_scales[e, 1:KP])
-            for s in range(1, KP):
-                load_w1(e, s)
-        w2 = keep.tile([P, E * HP, 2 * N], U8, name="w2", align_bytes=64)
-        nc.sync.dma_start(
-            out=w2[:].rearrange("p e b -> p (e b)").bitcast(I32).rearrange("p (e b) -> p e b", e=E * HP),
-            in_=w2_words.bitcast(I32).rearrange("e s p b -> p (e s) b"),
-        )
-        load_scales(w2s, w2_scales.rearrange("e s q i -> (e s) q i"))
+        load_scales(w1s[1], w1_scales[:, 1])
+        load_w1(0, 1)
+        load_w1(1, 1)
+        load_scales(w1s[2], w1_scales[:, 2])
+        load_w1(0, 2)
+        load_w2()
+        load_w1(1, 2)
         gates = keep.tile([P, E * C], F32, name="gates")
         nc.sync.dma_start(out=gates[:], in_=gate)
 
-        xw = [keep.tile([P, T], U32, name=f"xw{s}", align_bytes=64) for s in range(KP)]
         gw, gs, acc = {}, {}, {}
         for st in range(TILES):
             for g in range(HP):
@@ -132,25 +140,23 @@ def tile_moe_pln_mlp_silu_kernel(
                     in_=mixed[:, c0 : c0 + w, :].rearrange("p w j -> p (w j)"),
                 )
 
-        for e in range(E):
-            for s in range(KP):
-                gw[e, s] = keep.tile([P, C], U32, name=f"gw{e}_{s}", align_bytes=64)
-                gs[e, s] = keep.tile([P, C], U8, name=f"gs{e}_{s}", align_bytes=64)
-
-        def gather(e, s, lo, n):
-            o = (e * C + lo) // 16
-            idx = offsets[:, o : o + n // 16]
-            nc.vector.tensor_copy(gw[e, s][:, lo : lo + n], xw[s][:].indirect(idx))
-            nc.vector.tensor_copy(gs[e, s][:, lo : lo + n], xsc[s][:].indirect(idx))
+        def gather(s, lo, n):
+            idx = offsets[:, lo // 16 : (lo + n) // 16]
+            words = keep.tile([P, n], U32, name=f"gw{s}_{lo}", align_bytes=64)
+            planes = keep.tile([P, n], U8, name=f"gs{s}_{lo}", align_bytes=64)
+            nc.vector.tensor_copy(words[:], xw[s][:].indirect(idx))
+            nc.vector.tensor_copy(planes[:], xsc[s][:].indirect(idx))
+            for c0 in range(0, n, P):
+                gw[s, (lo + c0) // P] = words[:, c0 : c0 + P]
+                gs[s, (lo + c0) // P] = planes[:, c0 : c0 + P]
 
         def first_layer(st, s):
-            e, half = divmod(st, 2)
-            cols = slice(half * P, (half + 1) * P)
+            e = st // 2
             for g in range(HP):
                 nc.tensor.matmul_mx(
                     out=acc[st, g][:],
-                    lhsT=gw[e, s][:, cols].bitcast(FP8X4),
-                    lhsT_scale=gs[e, s][:, cols],
+                    lhsT=gw[s, st].bitcast(FP8X4),
+                    lhsT_scale=gs[s, st],
                     rhs=w1[e, s][:, g * 1024 : (g + 1) * 1024].bitcast(FP4X4),
                     rhs_scale=w1_scale(e, s, g),
                     start=(s == 0),
@@ -165,13 +171,13 @@ def tile_moe_pln_mlp_silu_kernel(
             else:
                 nc.vector.tensor_copy(dst, src)
 
-        def second_layer(st):
-            e = st // 2
-            hs = keep.tile([P, H], BF16, name=f"hs{st}", align_bytes=64)
-            words = hs[:].bitcast(F32)
+        turned, sums = {}, {}
+
+        def activate(st):
+            hs = [keep.tile([P, 512], BF16, name=f"hs{st}_{g}", align_bytes=64) for g in range(HP)]
             for g in range(HP):
                 nc.scalar.activation(
-                    hs[:, g * 512 : (g + 1) * 512].rearrange("p (u m d) -> p u m d", u=2, d=2),
+                    hs[g][:].rearrange("p (u m d) -> p u m d", u=2, d=2),
                     acc[st, g][:].rearrange("p (m u d) -> p u m d", u=2, d=2),
                     SILU,
                 )
@@ -179,9 +185,13 @@ def tile_moe_pln_mlp_silu_kernel(
             for g in range(HP):
                 tp = psum.tile([P, 512], F32, name=f"tp{st}_{g}", tag=f"bank{2 * st + g}")
                 for u in range(2):
-                    b = 2 * g + u
-                    nc.tensor.transpose(tp[:, u * P : (u + 1) * P], words[:, b * P : (b + 1) * P], ident[:])
+                    nc.tensor.transpose(tp[:, u * P : (u + 1) * P], hs[g][:].bitcast(F32)[:, u * P : (u + 1) * P], ident[:])
                 tps.append(tp)
+            turned[st] = tps
+
+        def second_layer(st):
+            e = st // 2
+            tps = turned[st]
             y = psum.tile([P, 512], F32, name=f"y{st}", tag=f"bank{2 * st}")
             hb = keep.tile([P, HP * 512], BF16, name=f"hb{st}", align_bytes=64)
             hw = keep.tile([P, HP * P], U32, name=f"hw{st}", align_bytes=64)
@@ -190,7 +200,7 @@ def tile_moe_pln_mlp_silu_kernel(
                 dst = hb[:, g * 512 : (g + 1) * 512].bitcast(F32).rearrange("p (r u) -> p r u", u=2)
                 src = tps[g][:, 0 : 2 * P].rearrange("p (u r) -> p r u", u=2)
                 move(TURN[st][g], dst, src)
-            step = 1 if st == TILES - 1 else HP
+            step = 1 if st in SPLIT else HP
             for g0 in range(0, HP, step):
                 nc.vector.quantize_mx(
                     out=hw[:, g0 * P : (g0 + step) * P].bitcast(FP8X4),
@@ -208,33 +218,42 @@ def tile_moe_pln_mlp_silu_kernel(
                         start=(g == 0),
                         stop=(g == HP - 1),
                     )
+            sums[st] = y
+
+        def leave(st):
             yt = keep.tile([P, P], F32, name=f"yt{st}")
-            move(YCOPY[st], yt[:], y[:, 0:P])
+            move(YCOPY[st], yt[:], sums[st][:, 0:P])
             ys[st] = yt
 
         for s in range(KP):
             quantise_x(s)
-        for e in range(E):
-            gather(e, 0, 0, C)
-            first_layer(2 * e, 0)
-            first_layer(2 * e + 1, 0)
-        gather(0, 1, 0, C)
+        gather(0, 0, E * C)
+        for st in range(TILES):
+            first_layer(st, 0)
+        gather(1, 0, E * C)
         first_layer(0, 1)
         first_layer(1, 1)
-        for half in range(2):
-            gather(0, 2, half * P, P)
-            first_layer(half, 2)
-        gather(1, 1, 0, C)
+        for st in range(2):
+            gather(2, st * P, P)
+            first_layer(st, 2)
+        for st in range(2, TILES):
+            gather(2, st * P, P)
         first_layer(2, 1)
-        first_layer(3, 1)
-        for half in range(2):
-            gather(1, 2, half * P, P)
-        second_layer(0)
         first_layer(2, 2)
-        second_layer(1)
+        activate(0)
+        first_layer(3, 1)
         first_layer(3, 2)
+        activate(1)
+        second_layer(0)
+        activate(2)
+        second_layer(1)
+        leave(0)
+        activate(3)
         second_layer(2)
+        leave(1)
         second_layer(3)
+        leave(2)
+        leave(3)
         for st in range(TILES):
             nc.vector.tensor_tensor(
                 result[:].indirect(offsets[:, st * 8 : (st + 1) * 8]), ys[st][:], gates[:, st * P : (st + 1) * P], MULT

@@ -23,12 +23,14 @@ LIST_COLS = E * C // 16
 TILES = E * C // P
 FLOPS = 2 * E * C * (K * H + H * N)
 
-SCALAR_TOKENS = (256, 512, 448)
+SCALAR_TOKENS = (256, 576, 512)
 QUANTS = ((0, 512), (512, 128))
 TURN = ("vv", "vv", "ss", "ss")
 YCOPY = "vsss"
 WIDE = 704
-SPLIT = (2, 3,)
+EARLY = 4
+WARM = 6
+SPLIT = (3,)
 
 
 def tile_moe_pln_mlp_silu_kernel(
@@ -42,11 +44,14 @@ def tile_moe_pln_mlp_silu_kernel(
 
         offsets = lists.tile([P, LIST_COLS], U16, name="offsets")
 
-        w1s = [keep.tile([P, E * H], U8, name=f"w1s{s}", align_bytes=64) for s in range(KP)]
+        early_scales = keep.tile([P, EARLY * H], U8, name="w1s_early", align_bytes=64)
+        late_scales = keep.tile([P, (E * KP - EARLY) * H], U8, name="w1s_late", align_bytes=64)
         w2s = keep.tile([P, E * HP * N], U8, name="w2s", align_bytes=64)
-        nc.gpsimd.memset(w1s[0][:].bitcast(I32), 0)
-        for plane in w1s[1:] + [w2s]:
+        nc.gpsimd.memset(early_scales[:, 0 : EARLY * H // 2].bitcast(I32), 0)
+        nc.vector.memset(early_scales[:, EARLY * H // 2 : EARLY * H].bitcast(I32), 0)
+        for plane in (late_scales, w2s):
             nc.vector.memset(plane[:].bitcast(I32), 0)
+        w1_rows = w1_scales.rearrange("e s q i -> (e s) q i")
 
         warm = keep.tile([P, 1], F32, name="warm")
         nc.vector.memset(warm[:], 0.0)
@@ -94,29 +99,31 @@ def tile_moe_pln_mlp_silu_kernel(
                 out=w2[:].rearrange("p e b -> p (e b)").bitcast(I32).rearrange("p (e b) -> p e b", e=E * HP),
                 in_=w2_words.bitcast(I32).rearrange("e s p b -> p (e s) b"),
             )
-            load_scales(w2s, w2_scales.rearrange("e s q i -> (e s) q i"))
 
         def w1_scale(e, s, g):
-            return w1s[s][:, e * H + g * 512 : e * H + (g + 1) * 512]
+            block = e * KP + s
+            if block < EARLY:
+                return early_scales[:, block * H + g * 512 : block * H + (g + 1) * 512]
+            return late_scales[:, (block - EARLY) * H + g * 512 : (block - EARLY) * H + (g + 1) * 512]
 
         load_x(0)
         nc.sync.dma_start(offsets[:], offs)
         load_x(1)
-        load_scales(w1s[0], w1_scales[:, 0])
+        load_x(2)
+        load_scales(early_scales, w1_rows[0:EARLY])
         load_w1(0, 0)
         load_w1(1, 0)
-        load_x(2)
-        load_scales(w1s[1], w1_scales[:, 1])
         load_w1(0, 1)
-        load_w1(1, 1)
-        load_scales(w1s[2], w1_scales[:, 2])
+        load_scales(late_scales, w1_rows[EARLY : E * KP])
         load_w1(0, 2)
-        load_w2()
+        load_w1(1, 1)
         load_w1(1, 2)
+        load_w2()
         gates = keep.tile([P, E * C], F32, name="gates")
         nc.sync.dma_start(out=gates[:], in_=gate)
+        load_scales(w2s, w2_scales.rearrange("e s q i -> (e s) q i"))
 
-        gw, gs, acc = {}, {}, {}
+        gw, gs, acc, whole = {}, {}, {}, {}
         for st in range(TILES):
             for g in range(HP):
                 acc[st, g] = psum.tile([P, 512], F32, name=f"acc{st}_{g}", tag=f"bank{2 * st + g}")
@@ -146,6 +153,7 @@ def tile_moe_pln_mlp_silu_kernel(
             planes = keep.tile([P, n], U8, name=f"gs{s}_{lo}", align_bytes=64)
             nc.vector.tensor_copy(words[:], xw[s][:].indirect(idx))
             nc.vector.tensor_copy(planes[:], xsc[s][:].indirect(idx))
+            whole[s] = (words, planes)
             for c0 in range(0, n, P):
                 gw[s, (lo + c0) // P] = words[:, c0 : c0 + P]
                 gs[s, (lo + c0) // P] = planes[:, c0 : c0 + P]
@@ -161,6 +169,19 @@ def tile_moe_pln_mlp_silu_kernel(
                     rhs_scale=w1_scale(e, s, g),
                     start=(s == 0),
                     stop=(s == KP - 1),
+                )
+
+        def warm_up():
+            words, planes = whole[0]
+            for turn in range(WARM):
+                nc.tensor.matmul_mx(
+                    out=acc[TILES - 1, HP - 1][:],
+                    lhsT=gw[0, 0].bitcast(FP8X4),
+                    lhsT_scale=gs[0, 0],
+                    rhs=words[:, 0:256].bitcast(U8).bitcast(FP4X4),
+                    rhs_scale=planes[:],
+                    start=True,
+                    stop=True,
                 )
 
         ys = {}
@@ -228,6 +249,7 @@ def tile_moe_pln_mlp_silu_kernel(
         for s in range(KP):
             quantise_x(s)
         gather(0, 0, E * C)
+        warm_up()
         for st in range(TILES):
             first_layer(st, 0)
         gather(1, 0, E * C)

@@ -23,14 +23,14 @@ LIST_COLS = E * C // 16
 TILES = E * C // P
 FLOPS = 2 * E * C * (K * H + H * N)
 
-SCALAR_TOKENS = (256, 576, 512)
+SCALAR_TOKENS = (256, 512, 448)
 QUANTS = ((0, 512), (512, 128))
-TURN = ("vv", "vv", "ss", "ss")
-YCOPY = "vsss"
+TURN = ("vv", "vv", "vv", "ss")
+YCOPY = "sssv"
 WIDE = 704
-EARLY = 4
-WARM = 6
-SPLIT = (3,)
+EARLY = 3
+WARM = 12
+SPLIT = (0, 1, 2, 3,)
 
 
 def tile_moe_pln_mlp_silu_kernel(
@@ -40,6 +40,7 @@ def tile_moe_pln_mlp_silu_kernel(
     with ExitStack() as ctx:
         lists = ctx.enter_context(tc.tile_pool(name="lists", bufs=1))
         keep = ctx.enter_context(tc.tile_pool(name="keep", bufs=1))
+        shared = ctx.enter_context(tc.tile_pool(name="shared", bufs=1))
         psum = ctx.enter_context(tc.psum_pool(name="psum", bufs=1))
 
         offsets = lists.tile([P, LIST_COLS], U16, name="offsets")
@@ -100,6 +101,14 @@ def tile_moe_pln_mlp_silu_kernel(
                 in_=w2_words.bitcast(I32).rearrange("e s p b -> p (e s) b"),
             )
 
+        gates = keep.tile([P, E * C], F32, name="gates")
+
+        def load_gate():
+            nc.sync.dma_start(out=gates[:], in_=gate)
+
+        def load_w2_scales():
+            load_scales(w2s, w2_scales.rearrange("e s q i -> (e s) q i"))
+
         def w1_scale(e, s, g):
             block = e * KP + s
             if block < EARLY:
@@ -112,16 +121,15 @@ def tile_moe_pln_mlp_silu_kernel(
         load_x(2)
         load_scales(early_scales, w1_rows[0:EARLY])
         load_w1(0, 0)
-        load_w1(1, 0)
         load_w1(0, 1)
+        load_w1(1, 0)
         load_scales(late_scales, w1_rows[EARLY : E * KP])
         load_w1(0, 2)
+        load_w2()
+        load_w2_scales()
         load_w1(1, 1)
         load_w1(1, 2)
-        load_w2()
-        gates = keep.tile([P, E * C], F32, name="gates")
-        nc.sync.dma_start(out=gates[:], in_=gate)
-        load_scales(w2s, w2_scales.rearrange("e s q i -> (e s) q i"))
+        load_gate()
 
         gw, gs, acc, whole = {}, {}, {}, {}
         for st in range(TILES):
@@ -137,7 +145,10 @@ def tile_moe_pln_mlp_silu_kernel(
             nc.scalar.activation(dst, src, COPY)
 
         def quantise_x(s):
-            mixed = keep.tile([P, T, 4], BF16, name=f"xb{s}", align_bytes=64)
+            if s == KP - 1:
+                mixed = shared.tile([P, T, 4], BF16, name=f"xb{s}", align_bytes=64, offset=0)
+            else:
+                mixed = keep.tile([P, T, 4], BF16, name=f"xb{s}", align_bytes=64)
             round_x(mixed, s, 0, SCALAR_TOKENS[s], scalar_round)
             round_x(mixed, s, SCALAR_TOKENS[s], T, nc.vector.tensor_copy)
             for c0, w in QUANTS:
@@ -147,10 +158,14 @@ def tile_moe_pln_mlp_silu_kernel(
                     in_=mixed[:, c0 : c0 + w, :].rearrange("p w j -> p (w j)"),
                 )
 
-        def gather(s, lo, n):
+        def gather(s, lo, n, late=False):
             idx = offsets[:, lo // 16 : (lo + n) // 16]
-            words = keep.tile([P, n], U32, name=f"gw{s}_{lo}", align_bytes=64)
-            planes = keep.tile([P, n], U8, name=f"gs{s}_{lo}", align_bytes=64)
+            if late:
+                words = shared.tile([P, n], U32, name=f"gw{s}_{lo}", align_bytes=64, offset=0)
+                planes = shared.tile([P, n], U8, name=f"gs{s}_{lo}", align_bytes=64, offset=4 * n)
+            else:
+                words = keep.tile([P, n], U32, name=f"gw{s}_{lo}", align_bytes=64)
+                planes = keep.tile([P, n], U8, name=f"gs{s}_{lo}", align_bytes=64)
             nc.vector.tensor_copy(words[:], xw[s][:].indirect(idx))
             nc.vector.tensor_copy(planes[:], xsc[s][:].indirect(idx))
             whole[s] = (words, planes)
@@ -175,10 +190,10 @@ def tile_moe_pln_mlp_silu_kernel(
             words, planes = whole[0]
             for turn in range(WARM):
                 nc.tensor.matmul_mx(
-                    out=acc[TILES - 1, HP - 1][:],
+                    out=acc[TILES - 1, HP - 1][:, 0:C],
                     lhsT=gw[0, 0].bitcast(FP8X4),
                     lhsT_scale=gs[0, 0],
-                    rhs=words[:, 0:256].bitcast(U8).bitcast(FP4X4),
+                    rhs=words[:, 0 : C // 2].bitcast(U8).bitcast(FP4X4),
                     rhs_scale=planes[:],
                     start=True,
                     stop=True,
@@ -248,29 +263,30 @@ def tile_moe_pln_mlp_silu_kernel(
 
         for s in range(KP):
             quantise_x(s)
-        gather(0, 0, E * C)
+        gather(0, 0, C)
         warm_up()
-        for st in range(TILES):
-            first_layer(st, 0)
-        gather(1, 0, E * C)
+        first_layer(0, 0)
+        first_layer(1, 0)
+        gather(0, C, C)
+        gather(1, 0, C)
         first_layer(0, 1)
         first_layer(1, 1)
         for st in range(2):
             gather(2, st * P, P)
             first_layer(st, 2)
-        for st in range(2, TILES):
-            gather(2, st * P, P)
-        first_layer(2, 1)
-        first_layer(2, 2)
+        gather(1, C, C, late=True)
+        gather(2, C, C)
         activate(0)
-        first_layer(3, 1)
-        first_layer(3, 2)
+        for s in range(KP):
+            first_layer(2, s)
         activate(1)
         second_layer(0)
+        for s in range(KP):
+            first_layer(3, s)
         activate(2)
         second_layer(1)
-        leave(0)
         activate(3)
+        leave(0)
         second_layer(2)
         leave(1)
         second_layer(3)

@@ -23,14 +23,14 @@ LIST_COLS = E * C // 16
 TILES = E * C // P
 FLOPS = 2 * E * C * (K * H + H * N)
 
-SCALAR_TOKENS = (256, 512, 448)
+SCALAR_TOKENS = (224, 512, 448)
 QUANTS = ((0, 512), (512, 128))
 TURN = ("vv", "vv", "vv", "ss")
 YCOPY = "sssv"
 WIDE = 704
-EARLY = 3
+EARLY = 2
 WARM = 12
-SPLIT = (0, 1, 2, 3,)
+SPLIT = (2, 3,)
 
 
 def tile_moe_pln_mlp_silu_kernel(
@@ -122,14 +122,14 @@ def tile_moe_pln_mlp_silu_kernel(
         load_scales(early_scales, w1_rows[0:EARLY])
         load_w1(0, 0)
         load_w1(0, 1)
-        load_w1(1, 0)
         load_scales(late_scales, w1_rows[EARLY : E * KP])
         load_w1(0, 2)
-        load_w2()
-        load_w2_scales()
+        load_w1(1, 0)
         load_w1(1, 1)
         load_w1(1, 2)
+        load_w2()
         load_gate()
+        load_w2_scales()
 
         gw, gs, acc, whole = {}, {}, {}, {}
         for st in range(TILES):
@@ -268,6 +268,8 @@ def tile_moe_pln_mlp_silu_kernel(
         first_layer(0, 0)
         first_layer(1, 0)
         gather(0, C, C)
+        first_layer(2, 0)
+        first_layer(3, 0)
         gather(1, 0, C)
         first_layer(0, 1)
         first_layer(1, 1)
@@ -277,12 +279,12 @@ def tile_moe_pln_mlp_silu_kernel(
         gather(1, C, C, late=True)
         gather(2, C, C)
         activate(0)
-        for s in range(KP):
-            first_layer(2, s)
+        first_layer(2, 1)
+        first_layer(2, 2)
         activate(1)
         second_layer(0)
-        for s in range(KP):
-            first_layer(3, s)
+        first_layer(3, 1)
+        first_layer(3, 2)
         activate(2)
         second_layer(1)
         activate(3)

@@ -27,7 +27,6 @@ SCALAR_TOKENS = (224, 512, 448)
 QUANTS = ((0, 512), (512, 128))
 TURN = ("vv", "vv", "vv", "ss")
 YCOPY = "sssv"
-WIDE = 704
 EARLY = 2
 WARM = 12
 SPLIT = (2, 3,)
@@ -54,18 +53,12 @@ def tile_moe_pln_mlp_silu_kernel(
             nc.vector.memset(plane[:].bitcast(I32), 0)
         w1_rows = w1_scales.rearrange("e s q i -> (e s) q i")
 
-        warm = keep.tile([P, 1], F32, name="warm")
-        nc.vector.memset(warm[:], 0.0)
-        nc.scalar.activation(warm[:], warm[:], SILU)
-
         xsc = []
         for s in range(KP):
-            t = keep.tile([P, WIDE], U8, name=f"xsc{s}", align_bytes=64)
+            t = keep.tile([P, T], U8, name=f"xsc{s}", align_bytes=64)
             nc.vector.memset(t[:].bitcast(I32), 0)
             xsc.append(t)
-        xw = [keep.tile([P, WIDE], U32, name=f"xw{s}", align_bytes=64) for s in range(KP)]
-        for s in range(KP):
-            nc.vector.memset(xw[s][:, T:WIDE].bitcast(I32), 0)
+        xw = [keep.tile([P, T], U32, name=f"xw{s}", align_bytes=64) for s in range(KP)]
         result = keep.tile([P, T], F32, name="result")
         nc.vector.memset(result[:], 0.0)
 

@@ -27,6 +27,7 @@ SCALAR_TOKENS = (224, 512, 448)
 QUANTS = ((0, 512), (512, 128))
 TURN = ("vv", "vv", "vv", "ss")
 YCOPY = "sssv"
+ALIGN = 256
 EARLY = 2
 WARM = 12
 SPLIT = (2, 3,)
@@ -44,9 +45,9 @@ def tile_moe_pln_mlp_silu_kernel(
 
         offsets = lists.tile([P, LIST_COLS], U16, name="offsets")
 
-        early_scales = keep.tile([P, EARLY * H], U8, name="w1s_early", align_bytes=64)
-        late_scales = keep.tile([P, (E * KP - EARLY) * H], U8, name="w1s_late", align_bytes=64)
-        w2s = keep.tile([P, E * HP * N], U8, name="w2s", align_bytes=64)
+        early_scales = keep.tile([P, EARLY * H], U8, name="w1s_early", align_bytes=ALIGN)
+        late_scales = keep.tile([P, (E * KP - EARLY) * H], U8, name="w1s_late", align_bytes=ALIGN)
+        w2s = keep.tile([P, E * HP * N], U8, name="w2s", align_bytes=ALIGN)
         nc.gpsimd.memset(early_scales[:, 0 : EARLY * H // 2].bitcast(I32), 0)
         nc.vector.memset(early_scales[:, EARLY * H // 2 : EARLY * H].bitcast(I32), 0)
         for plane in (late_scales, w2s):
@@ -55,21 +56,21 @@ def tile_moe_pln_mlp_silu_kernel(
 
         xsc = []
         for s in range(KP):
-            t = keep.tile([P, T], U8, name=f"xsc{s}", align_bytes=64)
+            t = keep.tile([P, T], U8, name=f"xsc{s}", align_bytes=ALIGN)
             nc.vector.memset(t[:].bitcast(I32), 0)
             xsc.append(t)
-        xw = [keep.tile([P, T], U32, name=f"xw{s}", align_bytes=64) for s in range(KP)]
-        result = keep.tile([P, T], F32, name="result")
+        xw = [keep.tile([P, T], U32, name=f"xw{s}", align_bytes=ALIGN) for s in range(KP)]
+        result = keep.tile([P, T], F32, name="result", align_bytes=ALIGN)
         nc.vector.memset(result[:], 0.0)
 
-        ident = keep.tile([P, P], F32, name="ident")
+        ident = keep.tile([P, P], F32, name="ident", align_bytes=ALIGN)
         make_identity(nc, ident[:])
 
         raw = {}
         w1 = {}
 
         def load_x(s):
-            raw[s] = keep.tile([P, 4, T], F32, name=f"raw{s}")
+            raw[s] = keep.tile([P, 4, T], F32, name=f"raw{s}", align_bytes=ALIGN)
             nc.sync.dma_start(
                 out=raw[s][:], in_=xT[512 * s : 512 * (s + 1), :].rearrange("(p j) w -> p j w", j=4)
             )
@@ -82,11 +83,11 @@ def tile_moe_pln_mlp_silu_kernel(
                 )
 
         def load_w1(e, s):
-            t = keep.tile([P, 2 * H], U8, name=f"w1_{e}_{s}", align_bytes=64)
+            t = keep.tile([P, 2 * H], U8, name=f"w1_{e}_{s}", align_bytes=ALIGN)
             nc.sync.dma_start(out=t[:].bitcast(I32), in_=w1_words[e, s].bitcast(I32))
             w1[e, s] = t
 
-        w2 = keep.tile([P, E * HP, 2 * N], U8, name="w2", align_bytes=64)
+        w2 = keep.tile([P, E * HP, 2 * N], U8, name="w2", align_bytes=ALIGN)
 
         def load_w2():
             nc.sync.dma_start(
@@ -94,7 +95,7 @@ def tile_moe_pln_mlp_silu_kernel(
                 in_=w2_words.bitcast(I32).rearrange("e s p b -> p (e s) b"),
             )
 
-        gates = keep.tile([P, E * C], F32, name="gates")
+        gates = keep.tile([P, E * C], F32, name="gates", align_bytes=ALIGN)
 
         def load_gate():
             nc.sync.dma_start(out=gates[:], in_=gate)
@@ -139,9 +140,9 @@ def tile_moe_pln_mlp_silu_kernel(
 
         def quantise_x(s):
             if s == KP - 1:
-                mixed = shared.tile([P, T, 4], BF16, name=f"xb{s}", align_bytes=64, offset=0)
+                mixed = shared.tile([P, T, 4], BF16, name=f"xb{s}", align_bytes=ALIGN, offset=0)
             else:
-                mixed = keep.tile([P, T, 4], BF16, name=f"xb{s}", align_bytes=64)
+                mixed = keep.tile([P, T, 4], BF16, name=f"xb{s}", align_bytes=ALIGN)
             round_x(mixed, s, 0, SCALAR_TOKENS[s], scalar_round)
             round_x(mixed, s, SCALAR_TOKENS[s], T, nc.vector.tensor_copy)
             for c0, w in QUANTS:
@@ -154,11 +155,11 @@ def tile_moe_pln_mlp_silu_kernel(
         def gather(s, lo, n, late=False):
             idx = offsets[:, lo // 16 : (lo + n) // 16]
             if late:
-                words = shared.tile([P, n], U32, name=f"gw{s}_{lo}", align_bytes=64, offset=0)
-                planes = shared.tile([P, n], U8, name=f"gs{s}_{lo}", align_bytes=64, offset=4 * n)
+                words = shared.tile([P, n], U32, name=f"gw{s}_{lo}", align_bytes=ALIGN, offset=0)
+                planes = shared.tile([P, n], U8, name=f"gs{s}_{lo}", align_bytes=ALIGN, offset=4 * n)
             else:
-                words = keep.tile([P, n], U32, name=f"gw{s}_{lo}", align_bytes=64)
-                planes = keep.tile([P, n], U8, name=f"gs{s}_{lo}", align_bytes=64)
+                words = keep.tile([P, n], U32, name=f"gw{s}_{lo}", align_bytes=ALIGN)
+                planes = keep.tile([P, n], U8, name=f"gs{s}_{lo}", align_bytes=ALIGN)
             nc.vector.tensor_copy(words[:], xw[s][:].indirect(idx))
             nc.vector.tensor_copy(planes[:], xsc[s][:].indirect(idx))
             whole[s] = (words, planes)
@@ -203,7 +204,7 @@ def tile_moe_pln_mlp_silu_kernel(
         turned, sums = {}, {}
 
         def activate(st):
-            hs = [keep.tile([P, 512], BF16, name=f"hs{st}_{g}", align_bytes=64) for g in range(HP)]
+            hs = [keep.tile([P, 512], BF16, name=f"hs{st}_{g}", align_bytes=ALIGN) for g in range(HP)]
             for g in range(HP):
                 nc.scalar.activation(
                     hs[g][:].rearrange("p (u m d) -> p u m d", u=2, d=2),
@@ -222,9 +223,9 @@ def tile_moe_pln_mlp_silu_kernel(
             e = st // 2
             tps = turned[st]
             y = psum.tile([P, 512], F32, name=f"y{st}", tag=f"bank{2 * st}")
-            hb = keep.tile([P, HP * 512], BF16, name=f"hb{st}", align_bytes=64)
-            hw = keep.tile([P, HP * P], U32, name=f"hw{st}", align_bytes=64)
-            hc = keep.tile([P, HP * P], U8, name=f"hc{st}", align_bytes=64)
+            hb = keep.tile([P, HP * 512], BF16, name=f"hb{st}", align_bytes=ALIGN)
+            hw = keep.tile([P, HP * P], U32, name=f"hw{st}", align_bytes=ALIGN)
+            hc = keep.tile([P, HP * P], U8, name=f"hc{st}", align_bytes=ALIGN)
             for g in range(HP):
                 dst = hb[:, g * 512 : (g + 1) * 512].bitcast(F32).rearrange("p (r u) -> p r u", u=2)
                 src = tps[g][:, 0 : 2 * P].rearrange("p (u r) -> p r u", u=2)
@@ -250,7 +251,7 @@ def tile_moe_pln_mlp_silu_kernel(
             sums[st] = y
 
         def leave(st):
-            yt = keep.tile([P, P], F32, name=f"yt{st}")
+            yt = keep.tile([P, P], F32, name=f"yt{st}", align_bytes=ALIGN)
             move(YCOPY[st], yt[:], sums[st][:, 0:P])
             ys[st] = yt
 

@@ -29,7 +29,6 @@ TURN = ("vv", "vv", "vv", "ss")
 YCOPY = "sssv"
 ALIGN = 256
 EARLY = 2
-WARM = 12
 SPLIT = (2, 3,)
 
 
@@ -125,7 +124,7 @@ def tile_moe_pln_mlp_silu_kernel(
         load_gate()
         load_w2_scales()
 
-        gw, gs, acc, whole = {}, {}, {}, {}
+        gw, gs, acc = {}, {}, {}
         for st in range(TILES):
             for g in range(HP):
                 acc[st, g] = psum.tile([P, 512], F32, name=f"acc{st}_{g}", tag=f"bank{2 * st + g}")
@@ -162,7 +161,6 @@ def tile_moe_pln_mlp_silu_kernel(
                 planes = keep.tile([P, n], U8, name=f"gs{s}_{lo}", align_bytes=ALIGN)
             nc.vector.tensor_copy(words[:], xw[s][:].indirect(idx))
             nc.vector.tensor_copy(planes[:], xsc[s][:].indirect(idx))
-            whole[s] = (words, planes)
             for c0 in range(0, n, P):
                 gw[s, (lo + c0) // P] = words[:, c0 : c0 + P]
                 gs[s, (lo + c0) // P] = planes[:, c0 : c0 + P]
@@ -178,19 +176,6 @@ def tile_moe_pln_mlp_silu_kernel(
                     rhs_scale=w1_scale(e, s, g),
                     start=(s == 0),
                     stop=(s == KP - 1),
-                )
-
-        def warm_up():
-            words, planes = whole[0]
-            for turn in range(WARM):
-                nc.tensor.matmul_mx(
-                    out=acc[TILES - 1, HP - 1][:, 0:C],
-                    lhsT=gw[0, 0].bitcast(FP8X4),
-                    lhsT_scale=gs[0, 0],
-                    rhs=words[:, 0 : C // 2].bitcast(U8).bitcast(FP4X4),
-                    rhs_scale=planes[:],
-                    start=True,
-                    stop=True,
                 )
 
         ys = {}
@@ -258,7 +243,6 @@ def tile_moe_pln_mlp_silu_kernel(
         for s in range(KP):
             quantise_x(s)
         gather(0, 0, C)
-        warm_up()
         first_layer(0, 0)
         first_layer(1, 0)
         gather(0, C, C)

@@ -23,13 +23,13 @@ LIST_COLS = E * C // 16
 TILES = E * C // P
 FLOPS = 2 * E * C * (K * H + H * N)
 
-SCALAR_TOKENS = (224, 512, 448)
+SCALAR_TOKENS = (224, 288, 320)
 QUANTS = ((0, 512), (512, 128))
-TURN = ("vv", "vv", "vv", "ss")
-YCOPY = "sssv"
+TURN = ("ss", "ss", "vs", "ss")
+YCOPY = "vsss"
 ALIGN = 256
 EARLY = 2
-SPLIT = (2, 3,)
+SPLIT = (0, 1, 2, 3)
 
 
 def tile_moe_pln_mlp_silu_kernel(
@@ -154,8 +154,9 @@ def tile_moe_pln_mlp_silu_kernel(
         def gather(s, lo, n, late=False):
             idx = offsets[:, lo // 16 : (lo + n) // 16]
             if late:
-                words = shared.tile([P, n], U32, name=f"gw{s}_{lo}", align_bytes=ALIGN, offset=0)
-                planes = shared.tile([P, n], U8, name=f"gs{s}_{lo}", align_bytes=ALIGN, offset=4 * n)
+                place = 1024 * (2 * ((lo - C) // P) + s)
+                words = shared.tile([P, n], U32, name=f"gw{s}_{lo}", align_bytes=ALIGN, offset=place)
+                planes = shared.tile([P, n], U8, name=f"gs{s}_{lo}", align_bytes=ALIGN, offset=place + 4 * n)
             else:
                 words = keep.tile([P, n], U32, name=f"gw{s}_{lo}", align_bytes=ALIGN)
                 planes = keep.tile([P, n], U8, name=f"gs{s}_{lo}", align_bytes=ALIGN)
@@ -186,7 +187,7 @@ def tile_moe_pln_mlp_silu_kernel(
             else:
                 nc.vector.tensor_copy(dst, src)
 
-        turned, sums = {}, {}
+        hidden, turned, sums = {}, {}, {}
 
         def activate(st):
             hs = [keep.tile([P, 512], BF16, name=f"hs{st}_{g}", align_bytes=ALIGN) for g in range(HP)]
@@ -196,24 +197,35 @@ def tile_moe_pln_mlp_silu_kernel(
                     acc[st, g][:].rearrange("p (m u d) -> p u m d", u=2, d=2),
                     SILU,
                 )
+            hidden[st] = hs
+
+        def transpose(st):
             tps = []
+            if st == 0:
+                both = psum.tile([P, 512], F32, name="tp0", tag="bank2")
             for g in range(HP):
-                tp = psum.tile([P, 512], F32, name=f"tp{st}_{g}", tag=f"bank{2 * st + g}")
+                if st == 0:
+                    tp = both[:, g * 2 * P : (g + 1) * 2 * P]
+                else:
+                    bank = 0 if (st, g) == (1, 0) else 2 * st + g
+                    tp = psum.tile([P, 512], F32, name=f"tp{st}_{g}", tag=f"bank{bank}")[:, 0 : 2 * P]
                 for u in range(2):
-                    nc.tensor.transpose(tp[:, u * P : (u + 1) * P], hs[g][:].bitcast(F32)[:, u * P : (u + 1) * P], ident[:])
+                    nc.tensor.transpose(
+                        tp[:, u * P : (u + 1) * P], hidden[st][g][:].bitcast(F32)[:, u * P : (u + 1) * P], ident[:]
+                    )
                 tps.append(tp)
             turned[st] = tps
 
         def second_layer(st):
             e = st // 2
             tps = turned[st]
-            y = psum.tile([P, 512], F32, name=f"y{st}", tag=f"bank{2 * st}")
+            y = psum.tile([P, 512], F32, name=f"y{st}", tag=f"bank{(1, 0, 4, 6)[st]}")
             hb = keep.tile([P, HP * 512], BF16, name=f"hb{st}", align_bytes=ALIGN)
             hw = keep.tile([P, HP * P], U32, name=f"hw{st}", align_bytes=ALIGN)
             hc = keep.tile([P, HP * P], U8, name=f"hc{st}", align_bytes=ALIGN)
             for g in range(HP):
                 dst = hb[:, g * 512 : (g + 1) * 512].bitcast(F32).rearrange("p (r u) -> p r u", u=2)
-                src = tps[g][:, 0 : 2 * P].rearrange("p (u r) -> p r u", u=2)
+                src = tps[g].rearrange("p (u r) -> p r u", u=2)
                 move(TURN[st][g], dst, src)
             step = 1 if st in SPLIT else HP
             for g0 in range(0, HP, step):
@@ -242,30 +254,27 @@ def tile_moe_pln_mlp_silu_kernel(
 
         for s in range(KP):
             quantise_x(s)
-        gather(0, 0, C)
-        first_layer(0, 0)
-        first_layer(1, 0)
-        gather(0, C, C)
-        first_layer(2, 0)
-        first_layer(3, 0)
-        gather(1, 0, C)
-        first_layer(0, 1)
-        first_layer(1, 1)
-        for st in range(2):
-            gather(2, st * P, P)
-            first_layer(st, 2)
-        gather(1, C, C, late=True)
-        gather(2, C, C)
+        for s in range(KP):
+            gather(s, 0, C)
+            first_layer(0, s)
+            first_layer(1, s)
+        for st in range(2, TILES):
+            for s in range(KP):
+                gather(s, st * P, P, late=s < KP - 1)
         activate(0)
-        first_layer(2, 1)
-        first_layer(2, 2)
+        for s in range(KP):
+            first_layer(2, s)
         activate(1)
+        transpose(0)
+        transpose(1)
+        for s in range(KP):
+            first_layer(3, s)
         second_layer(0)
-        first_layer(3, 1)
-        first_layer(3, 2)
         activate(2)
+        transpose(2)
         second_layer(1)
         activate(3)
+        transpose(3)
         leave(0)
         second_layer(2)
         leave(1)

@@ -23,9 +23,9 @@ LIST_COLS = E * C // 16
 TILES = E * C // P
 FLOPS = 2 * E * C * (K * H + H * N)
 
-SCALAR_TOKENS = (224, 288, 320)
+SCALAR_TOKENS = (224, 352, 352)
 QUANTS = ((0, 512), (512, 128))
-TURN = ("ss", "ss", "vs", "ss")
+TURN = ("ss", "vv", "ss", "ss")
 YCOPY = "vsss"
 ALIGN = 256
 EARLY = 2
@@ -121,8 +121,8 @@ def tile_moe_pln_mlp_silu_kernel(
         load_w1(1, 1)
         load_w1(1, 2)
         load_w2()
-        load_gate()
         load_w2_scales()
+        load_gate()
 
         gw, gs, acc = {}, {}, {}
         for st in range(TILES):
@@ -255,7 +255,11 @@ def tile_moe_pln_mlp_silu_kernel(
         for s in range(KP):
             quantise_x(s)
         for s in range(KP):
-            gather(s, 0, C)
+            if s < KP - 1:
+                gather(s, 0, C)
+            else:
+                gather(s, 0, P)
+                gather(s, P, P)
             first_layer(0, s)
             first_layer(1, s)
         for st in range(2, TILES):

@@ -23,9 +23,9 @@ LIST_COLS = E * C // 16
 TILES = E * C // P
 FLOPS = 2 * E * C * (K * H + H * N)
 
-SCALAR_TOKENS = (224, 352, 352)
-QUANTS = ((0, 512), (512, 128))
-TURN = ("ss", "vv", "ss", "ss")
+SCALAR_TOKENS = (224, 416, 256)
+QUANTS = ((512, 128), (0, 512))
+TURN = ("vv", "vv", "ss", "ss")
 YCOPY = "vsss"
 ALIGN = 256
 EARLY = 2
@@ -111,13 +111,13 @@ def tile_moe_pln_mlp_silu_kernel(
         load_x(0)
         nc.sync.dma_start(offsets[:], offs)
         load_x(1)
-        load_x(2)
         load_scales(early_scales, w1_rows[0:EARLY])
         load_w1(0, 0)
+        load_x(2)
         load_w1(0, 1)
         load_scales(late_scales, w1_rows[EARLY : E * KP])
-        load_w1(0, 2)
         load_w1(1, 0)
+        load_w1(0, 2)
         load_w1(1, 1)
         load_w1(1, 2)
         load_w2()
@@ -143,7 +143,8 @@ def tile_moe_pln_mlp_silu_kernel(
             else:
                 mixed = keep.tile([P, T, 4], BF16, name=f"xb{s}", align_bytes=ALIGN)
             round_x(mixed, s, 0, SCALAR_TOKENS[s], scalar_round)
-            round_x(mixed, s, SCALAR_TOKENS[s], T, nc.vector.tensor_copy)
+            round_x(mixed, s, 512, T, nc.vector.tensor_copy)
+            round_x(mixed, s, SCALAR_TOKENS[s], 512, nc.vector.tensor_copy)
             for c0, w in QUANTS:
                 nc.vector.quantize_mx(
                     out=xw[s][:, c0 : c0 + w].bitcast(FP8X4),
@@ -201,14 +202,8 @@ def tile_moe_pln_mlp_silu_kernel(
 
         def transpose(st):
             tps = []
-            if st == 0:
-                both = psum.tile([P, 512], F32, name="tp0", tag="bank2")
             for g in range(HP):
-                if st == 0:
-                    tp = both[:, g * 2 * P : (g + 1) * 2 * P]
-                else:
-                    bank = 0 if (st, g) == (1, 0) else 2 * st + g
-                    tp = psum.tile([P, 512], F32, name=f"tp{st}_{g}", tag=f"bank{bank}")[:, 0 : 2 * P]
+                tp = psum.tile([P, 512], F32, name=f"tp{st}_{g}", tag=f"bank{2 * st + g}")[:, 0 : 2 * P]
                 for u in range(2):
                     nc.tensor.transpose(
                         tp[:, u * P : (u + 1) * P], hidden[st][g][:].bitcast(F32)[:, u * P : (u + 1) * P], ident[:]
@@ -219,7 +214,7 @@ def tile_moe_pln_mlp_silu_kernel(
         def second_layer(st):
             e = st // 2
             tps = turned[st]
-            y = psum.tile([P, 512], F32, name=f"y{st}", tag=f"bank{(1, 0, 4, 6)[st]}")
+            y = psum.tile([P, 512], F32, name=f"y{st}", tag=f"bank{2 * st}")
             hb = keep.tile([P, HP * 512], BF16, name=f"hb{st}", align_bytes=ALIGN)
             hw = keep.tile([P, HP * P], U32, name=f"hw{st}", align_bytes=ALIGN)
             hc = keep.tile([P, HP * P], U8, name=f"hc{st}", align_bytes=ALIGN)
@@ -260,18 +255,24 @@ def tile_moe_pln_mlp_silu_kernel(
             else:
                 gather(s, 0, P)
                 gather(s, P, P)
+        gather(0, C, C)
+        for st in range(2, TILES):
+            for s in range(1, KP):
+                gather(s, st * P, P, late=s < KP - 1)
+        for s in range(KP - 1):
             first_layer(0, s)
             first_layer(1, s)
-        for st in range(2, TILES):
-            for s in range(KP):
-                gather(s, st * P, P, late=s < KP - 1)
+        first_layer(2, 0)
+        first_layer(3, 0)
+        first_layer(0, KP - 1)
+        first_layer(1, KP - 1)
         activate(0)
-        for s in range(KP):
-            first_layer(2, s)
         activate(1)
+        for s in range(1, KP):
+            first_layer(2, s)
         transpose(0)
         transpose(1)
-        for s in range(KP):
+        for s in range(1, KP):
             first_layer(3, s)
         second_layer(0)
         activate(2)

@@ -23,12 +23,12 @@ LIST_COLS = E * C // 16
 TILES = E * C // P
 FLOPS = 2 * E * C * (K * H + H * N)
 
-SCALAR_TOKENS = (224, 416, 256)
+SCALAR_TOKENS = (224, 352, 352)
 QUANTS = ((512, 128), (0, 512))
-TURN = ("vv", "vv", "ss", "ss")
-YCOPY = "vsss"
+TURN = ("ss", "ss", "ss", "ss")
+YCOPY = "vvss"
 ALIGN = 256
-EARLY = 2
+RUN = 2
 SPLIT = (0, 1, 2, 3)
 
 
@@ -44,12 +44,11 @@ def tile_moe_pln_mlp_silu_kernel(
 
         offsets = lists.tile([P, LIST_COLS], U16, name="offsets")
 
-        early_scales = keep.tile([P, EARLY * H], U8, name="w1s_early", align_bytes=ALIGN)
-        late_scales = keep.tile([P, (E * KP - EARLY) * H], U8, name="w1s_late", align_bytes=ALIGN)
+        w1s = [keep.tile([P, RUN * H], U8, name=f"w1s{r}", align_bytes=ALIGN) for r in range(E * KP // RUN)]
         w2s = keep.tile([P, E * HP * N], U8, name="w2s", align_bytes=ALIGN)
-        nc.gpsimd.memset(early_scales[:, 0 : EARLY * H // 2].bitcast(I32), 0)
-        nc.vector.memset(early_scales[:, EARLY * H // 2 : EARLY * H].bitcast(I32), 0)
-        for plane in (late_scales, w2s):
+        nc.gpsimd.memset(w1s[0][:, 0 : RUN * H // 2].bitcast(I32), 0)
+        nc.vector.memset(w1s[0][:, RUN * H // 2 : RUN * H].bitcast(I32), 0)
+        for plane in w1s[1:] + [w2s]:
             nc.vector.memset(plane[:].bitcast(I32), 0)
         w1_rows = w1_scales.rearrange("e s q i -> (e s) q i")
 
@@ -104,24 +103,20 @@ def tile_moe_pln_mlp_silu_kernel(
 
         def w1_scale(e, s, g):
             block = e * KP + s
-            if block < EARLY:
-                return early_scales[:, block * H + g * 512 : block * H + (g + 1) * 512]
-            return late_scales[:, (block - EARLY) * H + g * 512 : (block - EARLY) * H + (g + 1) * 512]
+            first = block % RUN * H + g * 512
+            return w1s[block // RUN][:, first : first + 512]
 
         load_x(0)
         nc.sync.dma_start(offsets[:], offs)
         load_x(1)
-        load_scales(early_scales, w1_rows[0:EARLY])
-        load_w1(0, 0)
         load_x(2)
-        load_w1(0, 1)
-        load_scales(late_scales, w1_rows[EARLY : E * KP])
-        load_w1(1, 0)
-        load_w1(0, 2)
-        load_w1(1, 1)
-        load_w1(1, 2)
+        for r in range(E * KP // RUN):
+            if r == E * KP // RUN - 1:
+                load_w2_scales()
+            load_scales(w1s[r], w1_rows[r * RUN : (r + 1) * RUN])
+            for block in range(r * RUN, (r + 1) * RUN):
+                load_w1(block // KP, block % KP)
         load_w2()
-        load_w2_scales()
         load_gate()
 
         gw, gs, acc = {}, {}, {}
@@ -255,34 +250,35 @@ def tile_moe_pln_mlp_silu_kernel(
             else:
                 gather(s, 0, P)
                 gather(s, P, P)
-        gather(0, C, C)
+        for st in range(2, TILES):
+            gather(0, st * P, P, late=True)
         for st in range(2, TILES):
             for s in range(1, KP):
                 gather(s, st * P, P, late=s < KP - 1)
         for s in range(KP - 1):
             first_layer(0, s)
             first_layer(1, s)
-        first_layer(2, 0)
-        first_layer(3, 0)
         first_layer(0, KP - 1)
         first_layer(1, KP - 1)
         activate(0)
         activate(1)
-        for s in range(1, KP):
-            first_layer(2, s)
+        first_layer(2, 0)
+        first_layer(3, 0)
         transpose(0)
         transpose(1)
         for s in range(1, KP):
-            first_layer(3, s)
-        second_layer(0)
+            first_layer(2, s)
         activate(2)
-        transpose(2)
-        second_layer(1)
-        activate(3)
-        transpose(3)
+        second_layer(0)
         leave(0)
-        second_layer(2)
+        for s in range(1, KP):
+            first_layer(3, s)
+        activate(3)
+        second_layer(1)
         leave(1)
+        transpose(2)
+        transpose(3)
+        second_layer(2)
         second_layer(3)
         leave(2)
         leave(3)

@@ -23,7 +23,7 @@ LIST_COLS = E * C // 16
 TILES = E * C // P
 FLOPS = 2 * E * C * (K * H + H * N)
 
-SCALAR_TOKENS = (224, 352, 352)
+SCALAR_TOKENS = (208, 512, 512)
 QUANTS = ((512, 128), (0, 512))
 TURN = ("ss", "ss", "ss", "ss")
 YCOPY = "vvss"
@@ -69,9 +69,9 @@ def tile_moe_pln_mlp_silu_kernel(
 
         def load_x(s):
             raw[s] = keep.tile([P, 4, T], F32, name=f"raw{s}", align_bytes=ALIGN)
-            nc.sync.dma_start(
-                out=raw[s][:], in_=xT[512 * s : 512 * (s + 1), :].rearrange("(p j) w -> p j w", j=4)
-            )
+            rows = xT[512 * s : 512 * (s + 1), :].rearrange("(p j) w -> p j w", j=4)
+            for u in range(2):
+                nc.sync.dma_start(out=raw[s][:, 2 * u : 2 * u + 2, :], in_=rows[:, 2 * u : 2 * u + 2, :])
 
         def load_scales(plane, rows):
             for r in range(4):
@@ -129,6 +129,10 @@ def tile_moe_pln_mlp_silu_kernel(
             dst = mixed[:, c0:c1, :].rearrange("p (c i) j -> p c j i", i=4)
             copy(dst, src)
 
+        def round_pair(mixed, s, u, c0, c1, copy):
+            src = raw[s][:, 2 * u : 2 * u + 2, c0:c1].rearrange("p d w -> p w d")
+            copy(mixed[:, c0:c1, 2 * u : 2 * u + 2], src)
+
         def scalar_round(dst, src):
             nc.scalar.activation(dst, src, COPY)
 
@@ -137,9 +141,14 @@ def tile_moe_pln_mlp_silu_kernel(
                 mixed = shared.tile([P, T, 4], BF16, name=f"xb{s}", align_bytes=ALIGN, offset=0)
             else:
                 mixed = keep.tile([P, T, 4], BF16, name=f"xb{s}", align_bytes=ALIGN)
-            round_x(mixed, s, 0, SCALAR_TOKENS[s], scalar_round)
-            round_x(mixed, s, 512, T, nc.vector.tensor_copy)
-            round_x(mixed, s, SCALAR_TOKENS[s], 512, nc.vector.tensor_copy)
+            for u in range(2):
+                round_pair(mixed, s, u, 0, SCALAR_TOKENS[s], scalar_round)
+            if s == 0:
+                round_pair(mixed, s, 0, SCALAR_TOKENS[s], T, nc.vector.tensor_copy)
+                round_pair(mixed, s, 1, 512, T, nc.vector.tensor_copy)
+                round_pair(mixed, s, 1, SCALAR_TOKENS[s], 512, nc.vector.tensor_copy)
+            else:
+                round_x(mixed, s, 512, T, nc.vector.tensor_copy)
             for c0, w in QUANTS:
                 nc.vector.quantize_mx(
                     out=xw[s][:, c0 : c0 + w].bitcast(FP8X4),
@@ -250,8 +259,7 @@ def tile_moe_pln_mlp_silu_kernel(
             else:
                 gather(s, 0, P)
                 gather(s, P, P)
-        for st in range(2, TILES):
-            gather(0, st * P, P, late=True)
+        gather(0, C, C)
         for st in range(2, TILES):
             for s in range(1, KP):
                 gather(s, st * P, P, late=s < KP - 1)

@@ -23,7 +23,7 @@ LIST_COLS = E * C // 16
 TILES = E * C // P
 FLOPS = 2 * E * C * (K * H + H * N)
 
-SCALAR_TOKENS = (208, 512, 512)
+SCALAR_TOKENS = (208, 448, 208)
 QUANTS = ((512, 128), (0, 512))
 TURN = ("ss", "ss", "ss", "ss")
 YCOPY = "vvss"
@@ -67,11 +67,12 @@ def tile_moe_pln_mlp_silu_kernel(
         raw = {}
         w1 = {}
 
-        def load_x(s):
+        for s in range(KP):
             raw[s] = keep.tile([P, 4, T], F32, name=f"raw{s}", align_bytes=ALIGN)
+
+        def load_x(s, u):
             rows = xT[512 * s : 512 * (s + 1), :].rearrange("(p j) w -> p j w", j=4)
-            for u in range(2):
-                nc.sync.dma_start(out=raw[s][:, 2 * u : 2 * u + 2, :], in_=rows[:, 2 * u : 2 * u + 2, :])
+            nc.sync.dma_start(out=raw[s][:, 2 * u : 2 * u + 2, :], in_=rows[:, 2 * u : 2 * u + 2, :])
 
         def load_scales(plane, rows):
             for r in range(4):
@@ -106,16 +107,20 @@ def tile_moe_pln_mlp_silu_kernel(
             first = block % RUN * H + g * 512
             return w1s[block // RUN][:, first : first + 512]
 
-        load_x(0)
+        load_x(0, 0)
+        load_x(0, 1)
         nc.sync.dma_start(offsets[:], offs)
-        load_x(1)
-        load_x(2)
+        load_x(1, 0)
+        load_x(1, 1)
+        load_x(2, 0)
         for r in range(E * KP // RUN):
             if r == E * KP // RUN - 1:
                 load_w2_scales()
             load_scales(w1s[r], w1_rows[r * RUN : (r + 1) * RUN])
             for block in range(r * RUN, (r + 1) * RUN):
                 load_w1(block // KP, block % KP)
+                if block == 0:
+                    load_x(2, 1)
         load_w2()
         load_gate()
 
@@ -143,12 +148,13 @@ def tile_moe_pln_mlp_silu_kernel(
                 mixed = keep.tile([P, T, 4], BF16, name=f"xb{s}", align_bytes=ALIGN)
             for u in range(2):
                 round_pair(mixed, s, u, 0, SCALAR_TOKENS[s], scalar_round)
-            if s == 0:
+            if s != 1:
                 round_pair(mixed, s, 0, SCALAR_TOKENS[s], T, nc.vector.tensor_copy)
                 round_pair(mixed, s, 1, 512, T, nc.vector.tensor_copy)
                 round_pair(mixed, s, 1, SCALAR_TOKENS[s], 512, nc.vector.tensor_copy)
             else:
                 round_x(mixed, s, 512, T, nc.vector.tensor_copy)
+                round_x(mixed, s, SCALAR_TOKENS[s], 512, nc.vector.tensor_copy)
             for c0, w in QUANTS:
                 nc.vector.quantize_mx(
                     out=xw[s][:, c0 : c0 + w].bitcast(FP8X4),
@@ -259,7 +265,8 @@ def tile_moe_pln_mlp_silu_kernel(
             else:
                 gather(s, 0, P)
                 gather(s, P, P)
-        gather(0, C, C)
+        gather(0, C, P)
+        gather(0, C + P, P, late=True)
         for st in range(2, TILES):
             for s in range(1, KP):
                 gather(s, st * P, P, late=s < KP - 1)

@@ -17,19 +17,20 @@ MULT = mybir.AluOpType.mult
 
 P = 128
 K, T, E, C, H, N = 1536, 640, 2, 256, 1024, 128
-KP = K // 512
-HP = H // 512
-LIST_COLS = E * C // 16
-TILES = E * C // P
+PASS = 512
+K_PASSES = K // PASS
+H_PASSES = H // PASS
+LAST = K_PASSES - 1
+GROUPS = E * C // P
+SLABS = E * K_PASSES
+LIST_ROWS = 16
+ALIGN = 256
 FLOPS = 2 * E * C * (K * H + H * N)
 
-SCALAR_TOKENS = (208, 448, 208)
-QUANTS = ((512, 128), (0, 512))
-TURN = ("ss", "ss", "ss", "ss")
-YCOPY = "vvss"
-ALIGN = 256
+SCALAR_TOKENS = (224, 352, 208)
+WIDE = 512
 RUN = 2
-SPLIT = (0, 1, 2, 3)
+HELD_BYTES = 1024
 
 
 def tile_moe_pln_mlp_silu_kernel(
@@ -39,40 +40,41 @@ def tile_moe_pln_mlp_silu_kernel(
     with ExitStack() as ctx:
         lists = ctx.enter_context(tc.tile_pool(name="lists", bufs=1))
         keep = ctx.enter_context(tc.tile_pool(name="keep", bufs=1))
-        shared = ctx.enter_context(tc.tile_pool(name="shared", bufs=1))
+        reused = ctx.enter_context(tc.tile_pool(name="reused", bufs=1))
         psum = ctx.enter_context(tc.psum_pool(name="psum", bufs=1))
 
-        offsets = lists.tile([P, LIST_COLS], U16, name="offsets")
+        offsets = lists.tile([P, E * C // LIST_ROWS], U16, name="offsets")
 
-        w1s = [keep.tile([P, RUN * H], U8, name=f"w1s{r}", align_bytes=ALIGN) for r in range(E * KP // RUN)]
-        w2s = keep.tile([P, E * HP * N], U8, name="w2s", align_bytes=ALIGN)
-        nc.gpsimd.memset(w1s[0][:, 0 : RUN * H // 2].bitcast(I32), 0)
-        nc.vector.memset(w1s[0][:, RUN * H // 2 : RUN * H].bitcast(I32), 0)
-        for plane in w1s[1:] + [w2s]:
+        def entries(slot, count):
+            return offsets[:, slot // LIST_ROWS : (slot + count) // LIST_ROWS]
+
+        w1_planes = [keep.tile([P, RUN * H], U8, name=f"w1s{r}", align_bytes=ALIGN) for r in range(SLABS // RUN)]
+        w2_plane = keep.tile([P, E * H_PASSES * N], U8, name="w2s", align_bytes=ALIGN)
+        nc.gpsimd.memset(w1_planes[0][:, 0 : RUN * H // 2].bitcast(I32), 0)
+        nc.vector.memset(w1_planes[0][:, RUN * H // 2 : RUN * H].bitcast(I32), 0)
+        for plane in w1_planes[1:] + [w2_plane]:
             nc.vector.memset(plane[:].bitcast(I32), 0)
-        w1_rows = w1_scales.rearrange("e s q i -> (e s) q i")
+        token_planes = []
+        for s in range(K_PASSES):
+            plane = keep.tile([P, T], U8, name=f"xsc{s}", align_bytes=ALIGN)
+            nc.vector.memset(plane[:].bitcast(I32), 0)
+            token_planes.append(plane)
+        token_words = [keep.tile([P, T], U32, name=f"xw{s}", align_bytes=ALIGN) for s in range(K_PASSES)]
 
-        xsc = []
-        for s in range(KP):
-            t = keep.tile([P, T], U8, name=f"xsc{s}", align_bytes=ALIGN)
-            nc.vector.memset(t[:].bitcast(I32), 0)
-            xsc.append(t)
-        xw = [keep.tile([P, T], U32, name=f"xw{s}", align_bytes=ALIGN) for s in range(KP)]
         result = keep.tile([P, T], F32, name="result", align_bytes=ALIGN)
         nc.vector.memset(result[:], 0.0)
 
         ident = keep.tile([P, P], F32, name="ident", align_bytes=ALIGN)
         make_identity(nc, ident[:])
 
-        raw = {}
+        raw = [keep.tile([P, 4, T], F32, name=f"raw{s}", align_bytes=ALIGN) for s in range(K_PASSES)]
         w1 = {}
+        w2 = keep.tile([P, E * H_PASSES, 2 * N], U8, name="w2", align_bytes=ALIGN)
+        gates = keep.tile([P, E * C], F32, name="gates", align_bytes=ALIGN)
 
-        for s in range(KP):
-            raw[s] = keep.tile([P, 4, T], F32, name=f"raw{s}", align_bytes=ALIGN)
-
-        def load_x(s, u):
-            rows = xT[512 * s : 512 * (s + 1), :].rearrange("(p j) w -> p j w", j=4)
-            nc.sync.dma_start(out=raw[s][:, 2 * u : 2 * u + 2, :], in_=rows[:, 2 * u : 2 * u + 2, :])
+        def load_x(s, d0, d1):
+            rows = xT[PASS * s : PASS * (s + 1), :].rearrange("(p d) w -> p d w", d=4)
+            nc.sync.dma_start(out=raw[s][:, d0:d1, :], in_=rows[:, d0:d1, :])
 
         def load_scales(plane, rows):
             for r in range(4):
@@ -81,225 +83,192 @@ def tile_moe_pln_mlp_silu_kernel(
                     in_=rows[:, r:16:4, :].bitcast(I32).rearrange("s q i -> q s i"),
                 )
 
-        def load_w1(e, s):
-            t = keep.tile([P, 2 * H], U8, name=f"w1_{e}_{s}", align_bytes=ALIGN)
-            nc.sync.dma_start(out=t[:].bitcast(I32), in_=w1_words[e, s].bitcast(I32))
-            w1[e, s] = t
+        def load_slab(slab):
+            words = keep.tile([P, 2 * H], U8, name=f"w1_{slab}", align_bytes=ALIGN)
+            nc.sync.dma_start(out=words[:].bitcast(I32), in_=w1_words[slab // K_PASSES, slab % K_PASSES].bitcast(I32))
+            w1[slab] = words
 
-        w2 = keep.tile([P, E * HP, 2 * N], U8, name="w2", align_bytes=ALIGN)
-
-        def load_w2():
-            nc.sync.dma_start(
-                out=w2[:].rearrange("p e b -> p (e b)").bitcast(I32).rearrange("p (e b) -> p e b", e=E * HP),
-                in_=w2_words.bitcast(I32).rearrange("e s p b -> p (e s) b"),
-            )
-
-        gates = keep.tile([P, E * C], F32, name="gates", align_bytes=ALIGN)
-
-        def load_gate():
-            nc.sync.dma_start(out=gates[:], in_=gate)
-
-        def load_w2_scales():
-            load_scales(w2s, w2_scales.rearrange("e s q i -> (e s) q i"))
-
-        def w1_scale(e, s, g):
-            block = e * KP + s
-            first = block % RUN * H + g * 512
-            return w1s[block // RUN][:, first : first + 512]
-
-        load_x(0, 0)
-        load_x(0, 1)
+        load_x(0, 0, 4)
         nc.sync.dma_start(offsets[:], offs)
-        load_x(1, 0)
-        load_x(1, 1)
-        load_x(2, 0)
-        for r in range(E * KP // RUN):
-            if r == E * KP // RUN - 1:
-                load_w2_scales()
-            load_scales(w1s[r], w1_rows[r * RUN : (r + 1) * RUN])
-            for block in range(r * RUN, (r + 1) * RUN):
-                load_w1(block // KP, block % KP)
-                if block == 0:
-                    load_x(2, 1)
-        load_w2()
-        load_gate()
+        load_x(1, 0, 4)
+        load_x(LAST, 0, 2)
+        w1_rows = w1_scales.rearrange("e s q i -> (e s) q i")
+        for r in range(SLABS // RUN):
+            if r == SLABS // RUN - 1:
+                load_scales(w2_plane, w2_scales.rearrange("e s q i -> (e s) q i"))
+            load_scales(w1_planes[r], w1_rows[r * RUN : (r + 1) * RUN])
+            for slab in range(r * RUN, (r + 1) * RUN):
+                load_slab(slab)
+                if slab == 0:
+                    load_x(LAST, 2, 4)
+        nc.sync.dma_start(
+            out=w2[:].rearrange("p e b -> p (e b)").bitcast(I32).rearrange("p (e b) -> p e b", e=E * H_PASSES),
+            in_=w2_words.bitcast(I32).rearrange("e s p b -> p (e s) b"),
+        )
+        nc.sync.dma_start(out=gates[:], in_=gate)
 
-        gw, gs, acc = {}, {}, {}
-        for st in range(TILES):
-            for g in range(HP):
-                acc[st, g] = psum.tile([P, 512], F32, name=f"acc{st}_{g}", tag=f"bank{2 * st + g}")
+        def bank(group, g, name):
+            return psum.tile([P, PASS], F32, name=f"{name}{group}_{g}", tag=f"bank{H_PASSES * group + g}")
 
-        def round_x(mixed, s, c0, c1, copy):
-            src = raw[s][:, :, c0:c1].rearrange("p j (c i) -> p c j i", i=4)
-            dst = mixed[:, c0:c1, :].rearrange("p (c i) j -> p c j i", i=4)
-            copy(dst, src)
-
-        def round_pair(mixed, s, u, c0, c1, copy):
-            src = raw[s][:, 2 * u : 2 * u + 2, c0:c1].rearrange("p d w -> p w d")
-            copy(mixed[:, c0:c1, 2 * u : 2 * u + 2], src)
+        acc = {(group, g): bank(group, g, "acc") for group in range(GROUPS) for g in range(H_PASSES)}
 
         def scalar_round(dst, src):
             nc.scalar.activation(dst, src, COPY)
 
-        def quantise_x(s):
-            if s == KP - 1:
-                mixed = shared.tile([P, T, 4], BF16, name=f"xb{s}", align_bytes=ALIGN, offset=0)
+        def round_rows(rounded, s, t0, t1, copy):
+            src = raw[s][:, :, t0:t1].rearrange("p d (c i) -> p c d i", i=4)
+            copy(rounded[:, t0:t1, :].rearrange("p (c i) d -> p c d i", i=4), src)
+
+        def round_pair(rounded, s, u, t0, t1, copy):
+            src = raw[s][:, 2 * u : 2 * u + 2, t0:t1].rearrange("p d w -> p w d")
+            copy(rounded[:, t0:t1, 2 * u : 2 * u + 2], src)
+
+        def quantise_tokens(s):
+            if s == LAST:
+                rounded = reused.tile([P, T, 4], BF16, name=f"xb{s}", align_bytes=ALIGN, offset=0)
             else:
-                mixed = keep.tile([P, T, 4], BF16, name=f"xb{s}", align_bytes=ALIGN)
-            for u in range(2):
-                round_pair(mixed, s, u, 0, SCALAR_TOKENS[s], scalar_round)
-            if s != 1:
-                round_pair(mixed, s, 0, SCALAR_TOKENS[s], T, nc.vector.tensor_copy)
-                round_pair(mixed, s, 1, 512, T, nc.vector.tensor_copy)
-                round_pair(mixed, s, 1, SCALAR_TOKENS[s], 512, nc.vector.tensor_copy)
+                rounded = keep.tile([P, T, 4], BF16, name=f"xb{s}", align_bytes=ALIGN)
+            share = SCALAR_TOKENS[s]
+            if s == LAST:
+                round_pair(rounded, s, 0, 0, T, scalar_round)
+                round_pair(rounded, s, 1, 0, share, scalar_round)
+                round_pair(rounded, s, 1, WIDE, T, nc.vector.tensor_copy)
+                round_pair(rounded, s, 1, share, WIDE, nc.vector.tensor_copy)
             else:
-                round_x(mixed, s, 512, T, nc.vector.tensor_copy)
-                round_x(mixed, s, SCALAR_TOKENS[s], 512, nc.vector.tensor_copy)
-            for c0, w in QUANTS:
+                round_rows(rounded, s, 0, share, scalar_round)
+                round_rows(rounded, s, WIDE, T, nc.vector.tensor_copy)
+                round_rows(rounded, s, share, WIDE, nc.vector.tensor_copy)
+            for t0, t1 in ((WIDE, T), (0, WIDE)):
                 nc.vector.quantize_mx(
-                    out=xw[s][:, c0 : c0 + w].bitcast(FP8X4),
-                    scales=xsc[s][:, c0 : c0 + w],
-                    in_=mixed[:, c0 : c0 + w, :].rearrange("p w j -> p (w j)"),
+                    out=token_words[s][:, t0:t1].bitcast(FP8X4),
+                    scales=token_planes[s][:, t0:t1],
+                    in_=rounded[:, t0:t1, :].rearrange("p w d -> p (w d)"),
                 )
 
-        def gather(s, lo, n, late=False):
-            idx = offsets[:, lo // 16 : (lo + n) // 16]
-            if late:
-                place = 1024 * (2 * ((lo - C) // P) + s)
-                words = shared.tile([P, n], U32, name=f"gw{s}_{lo}", align_bytes=ALIGN, offset=place)
-                planes = shared.tile([P, n], U8, name=f"gs{s}_{lo}", align_bytes=ALIGN, offset=place + 4 * n)
-            else:
-                words = keep.tile([P, n], U32, name=f"gw{s}_{lo}", align_bytes=ALIGN)
-                planes = keep.tile([P, n], U8, name=f"gs{s}_{lo}", align_bytes=ALIGN)
-            nc.vector.tensor_copy(words[:], xw[s][:].indirect(idx))
-            nc.vector.tensor_copy(planes[:], xsc[s][:].indirect(idx))
-            for c0 in range(0, n, P):
-                gw[s, (lo + c0) // P] = words[:, c0 : c0 + P]
-                gs[s, (lo + c0) // P] = planes[:, c0 : c0 + P]
+        slot_words, slot_planes = {}, {}
 
-        def first_layer(st, s):
-            e = st // 2
-            for g in range(HP):
+        def gather(s, slot, count, held=False):
+            if held:
+                place = HELD_BYTES * (2 * ((slot - C) // P) + s)
+                words = reused.tile([P, count], U32, name=f"gw{s}_{slot}", align_bytes=ALIGN, offset=place)
+                planes = reused.tile([P, count], U8, name=f"gs{s}_{slot}", align_bytes=ALIGN, offset=place + 4 * count)
+            else:
+                words = keep.tile([P, count], U32, name=f"gw{s}_{slot}", align_bytes=ALIGN)
+                planes = keep.tile([P, count], U8, name=f"gs{s}_{slot}", align_bytes=ALIGN)
+            nc.vector.tensor_copy(words[:], token_words[s][:].indirect(entries(slot, count)))
+            nc.vector.tensor_copy(planes[:], token_planes[s][:].indirect(entries(slot, count)))
+            for c0 in range(0, count, P):
+                slot_words[s, (slot + c0) // P] = words[:, c0 : c0 + P]
+                slot_planes[s, (slot + c0) // P] = planes[:, c0 : c0 + P]
+
+        hidden, turned, sums, staged = {}, {}, {}, {}
+
+        def first_product(group, s):
+            slab = (group * P // C) * K_PASSES + s
+            for g in range(H_PASSES):
+                column = slab % RUN * H + g * PASS
                 nc.tensor.matmul_mx(
-                    out=acc[st, g][:],
-                    lhsT=gw[s, st].bitcast(FP8X4),
-                    lhsT_scale=gs[s, st],
-                    rhs=w1[e, s][:, g * 1024 : (g + 1) * 1024].bitcast(FP4X4),
-                    rhs_scale=w1_scale(e, s, g),
+                    out=acc[group, g][:],
+                    lhsT=slot_words[s, group].bitcast(FP8X4),
+                    lhsT_scale=slot_planes[s, group],
+                    rhs=w1[slab][:, 2 * g * PASS : 2 * (g + 1) * PASS].bitcast(FP4X4),
+                    rhs_scale=w1_planes[slab // RUN][:, column : column + PASS],
                     start=(s == 0),
-                    stop=(s == KP - 1),
+                    stop=(s == LAST),
                 )
 
-        ys = {}
-
-        def move(engine, dst, src):
-            if engine == "s":
-                nc.scalar.copy(dst, src)
-            else:
-                nc.vector.tensor_copy(dst, src)
-
-        hidden, turned, sums = {}, {}, {}
-
-        def activate(st):
-            hs = [keep.tile([P, 512], BF16, name=f"hs{st}_{g}", align_bytes=ALIGN) for g in range(HP)]
-            for g in range(HP):
+        def activate(group):
+            hidden[group] = [
+                keep.tile([P, PASS], BF16, name=f"hs{group}_{g}", align_bytes=ALIGN) for g in range(H_PASSES)
+            ]
+            for g in range(H_PASSES):
                 nc.scalar.activation(
-                    hs[g][:].rearrange("p (u m d) -> p u m d", u=2, d=2),
-                    acc[st, g][:].rearrange("p (m u d) -> p u m d", u=2, d=2),
+                    hidden[group][g][:].rearrange("p (u m d) -> p u m d", u=2, d=2),
+                    acc[group, g][:].rearrange("p (m u d) -> p u m d", u=2, d=2),
                     SILU,
                 )
-            hidden[st] = hs
 
-        def transpose(st):
-            tps = []
-            for g in range(HP):
-                tp = psum.tile([P, 512], F32, name=f"tp{st}_{g}", tag=f"bank{2 * st + g}")[:, 0 : 2 * P]
+        def turn(group):
+            turned[group] = []
+            for g in range(H_PASSES):
+                pairs = bank(group, g, "tp")[:, 0 : 2 * P]
                 for u in range(2):
-                    nc.tensor.transpose(
-                        tp[:, u * P : (u + 1) * P], hidden[st][g][:].bitcast(F32)[:, u * P : (u + 1) * P], ident[:]
-                    )
-                tps.append(tp)
-            turned[st] = tps
+                    run = slice(u * P, (u + 1) * P)
+                    nc.tensor.transpose(pairs[:, run], hidden[group][g][:].bitcast(F32)[:, run], ident[:])
+                turned[group].append(pairs)
 
-        def second_layer(st):
-            e = st // 2
-            tps = turned[st]
-            y = psum.tile([P, 512], F32, name=f"y{st}", tag=f"bank{2 * st}")
-            hb = keep.tile([P, HP * 512], BF16, name=f"hb{st}", align_bytes=ALIGN)
-            hw = keep.tile([P, HP * P], U32, name=f"hw{st}", align_bytes=ALIGN)
-            hc = keep.tile([P, HP * P], U8, name=f"hc{st}", align_bytes=ALIGN)
-            for g in range(HP):
-                dst = hb[:, g * 512 : (g + 1) * 512].bitcast(F32).rearrange("p (r u) -> p r u", u=2)
-                src = tps[g].rearrange("p (u r) -> p r u", u=2)
-                move(TURN[st][g], dst, src)
-            step = 1 if st in SPLIT else HP
-            for g0 in range(0, HP, step):
-                nc.vector.quantize_mx(
-                    out=hw[:, g0 * P : (g0 + step) * P].bitcast(FP8X4),
-                    scales=hc[:, g0 * P : (g0 + step) * P],
-                    in_=hb[:, g0 * 512 : (g0 + step) * 512],
+        def second_product(group):
+            sums[group] = bank(group, 0, "y")
+            values = keep.tile([P, H], BF16, name=f"hb{group}", align_bytes=ALIGN)
+            words = keep.tile([P, H_PASSES * P], U32, name=f"hw{group}", align_bytes=ALIGN)
+            planes = keep.tile([P, H_PASSES * P], U8, name=f"hc{group}", align_bytes=ALIGN)
+            for g in range(H_PASSES):
+                nc.scalar.copy(
+                    values[:, g * PASS : (g + 1) * PASS].bitcast(F32).rearrange("p (r u) -> p r u", u=2),
+                    turned[group][g].rearrange("p (u r) -> p r u", u=2),
                 )
-                for g in range(g0, g0 + step):
-                    row = e * HP + g
-                    nc.tensor.matmul_mx(
-                        out=y[:, 0:P],
-                        lhsT=w2[:, row, :].bitcast(FP4X4),
-                        lhsT_scale=w2s[:, row * N : (row + 1) * N],
-                        rhs=hw[:, g * P : (g + 1) * P].bitcast(FP8X4),
-                        rhs_scale=hc[:, g * P : (g + 1) * P],
-                        start=(g == 0),
-                        stop=(g == HP - 1),
-                    )
-            sums[st] = y
+            for g in range(H_PASSES):
+                nc.vector.quantize_mx(
+                    out=words[:, g * P : (g + 1) * P].bitcast(FP8X4),
+                    scales=planes[:, g * P : (g + 1) * P],
+                    in_=values[:, g * PASS : (g + 1) * PASS],
+                )
+                row = (group * P // C) * H_PASSES + g
+                nc.tensor.matmul_mx(
+                    out=sums[group][:, 0:P],
+                    lhsT=w2[:, row, :].bitcast(FP4X4),
+                    lhsT_scale=w2_plane[:, row * N : (row + 1) * N],
+                    rhs=words[:, g * P : (g + 1) * P].bitcast(FP8X4),
+                    rhs_scale=planes[:, g * P : (g + 1) * P],
+                    start=(g == 0),
+                    stop=(g == H_PASSES - 1),
+                )
 
-        def leave(st):
-            yt = keep.tile([P, P], F32, name=f"yt{st}", align_bytes=ALIGN)
-            move(YCOPY[st], yt[:], sums[st][:, 0:P])
-            ys[st] = yt
+        def stage(group, copy):
+            staged[group] = keep.tile([P, P], F32, name=f"yt{group}", align_bytes=ALIGN)
+            copy(staged[group][:], sums[group][:, 0:P])
 
-        for s in range(KP):
-            quantise_x(s)
-        for s in range(KP):
-            if s < KP - 1:
-                gather(s, 0, C)
-            else:
-                gather(s, 0, P)
-                gather(s, P, P)
-        gather(0, C, P)
-        gather(0, C + P, P, late=True)
-        for st in range(2, TILES):
-            for s in range(1, KP):
-                gather(s, st * P, P, late=s < KP - 1)
-        for s in range(KP - 1):
-            first_layer(0, s)
-            first_layer(1, s)
-        first_layer(0, KP - 1)
-        first_layer(1, KP - 1)
-        activate(0)
-        activate(1)
-        first_layer(2, 0)
-        first_layer(3, 0)
-        transpose(0)
-        transpose(1)
-        for s in range(1, KP):
-            first_layer(2, s)
-        activate(2)
-        second_layer(0)
-        leave(0)
-        for s in range(1, KP):
-            first_layer(3, s)
-        activate(3)
-        second_layer(1)
-        leave(1)
-        transpose(2)
-        transpose(3)
-        second_layer(2)
-        second_layer(3)
-        leave(2)
-        leave(3)
-        for st in range(TILES):
+        for s in range(K_PASSES):
+            quantise_tokens(s)
+
+        for s in range(LAST):
+            gather(s, 0, C)
+        for group in range(2):
+            gather(LAST, group * P, P)
+        gather(0, 2 * P, P)
+        gather(0, 3 * P, P, held=True)
+        for group in range(2, GROUPS):
+            for s in range(1, K_PASSES):
+                gather(s, group * P, P, held=s < LAST)
+
+        for s in range(K_PASSES):
+            for group in range(2):
+                first_product(group, s)
+        for group in range(2):
+            activate(group)
+        for group in range(2, GROUPS):
+            first_product(group, 0)
+        for group in range(2):
+            turn(group)
+        for group in range(2, GROUPS):
+            for s in range(1, K_PASSES):
+                first_product(group, s)
+            activate(group)
+            second_product(group - 2)
+            stage(group - 2, nc.vector.tensor_copy)
+        for group in range(2, GROUPS):
+            turn(group)
+        for group in range(2, GROUPS):
+            second_product(group)
+        for group in range(2, GROUPS):
+            stage(group, nc.scalar.copy)
+
+        for group in range(GROUPS):
             nc.vector.tensor_tensor(
-                result[:].indirect(offsets[:, st * 8 : (st + 1) * 8]), ys[st][:], gates[:, st * P : (st + 1) * P], MULT
+                result[:].indirect(entries(group * P, P)),
+                staged[group][:],
+                gates[:, group * P : (group + 1) * P],
+                MULT,
             )
 
         nc.sync.dma_start(out=out, in_=result[:])

@@ -27,10 +27,8 @@ LIST_ROWS = 16
 ALIGN = 256
 FLOPS = 2 * E * C * (K * H + H * N)
 
-SCALAR_TOKENS = (224, 352, 208)
-WIDE = 512
-RUN = 2
-HELD_BYTES = 1024
+SCALAR_TOKENS = {(0, 0): 224, (0, 1): 384, (K_PASSES - 1, 1): 320}
+RUNS = (slice(0, SLABS, K_PASSES), slice(1, K_PASSES), slice(K_PASSES + 1, SLABS))
 
 
 def tile_moe_pln_mlp_silu_kernel(
@@ -40,7 +38,7 @@ def tile_moe_pln_mlp_silu_kernel(
     with ExitStack() as ctx:
         lists = ctx.enter_context(tc.tile_pool(name="lists", bufs=1))
         keep = ctx.enter_context(tc.tile_pool(name="keep", bufs=1))
-        reused = ctx.enter_context(tc.tile_pool(name="reused", bufs=1))
+        late = ctx.enter_context(tc.tile_pool(name="late", bufs=2))
         psum = ctx.enter_context(tc.psum_pool(name="psum", bufs=1))
 
         offsets = lists.tile([P, E * C // LIST_ROWS], U16, name="offsets")
@@ -48,18 +46,16 @@ def tile_moe_pln_mlp_silu_kernel(
         def entries(slot, count):
             return offsets[:, slot // LIST_ROWS : (slot + count) // LIST_ROWS]
 
-        w1_planes = [keep.tile([P, RUN * H], U8, name=f"w1s{r}", align_bytes=ALIGN) for r in range(SLABS // RUN)]
+        w1_planes = [keep.tile([P, 2 * H], U8, name=f"w1s{r}", align_bytes=ALIGN) for r in range(len(RUNS))]
+        slab_plane = {}
+        for plane, run in zip(w1_planes, RUNS):
+            for n, slab in enumerate(range(SLABS)[run]):
+                slab_plane[slab] = plane[:, n * H : (n + 1) * H]
         w2_plane = keep.tile([P, E * H_PASSES * N], U8, name="w2s", align_bytes=ALIGN)
-        nc.gpsimd.memset(w1_planes[0][:, 0 : RUN * H // 2].bitcast(I32), 0)
-        nc.vector.memset(w1_planes[0][:, RUN * H // 2 : RUN * H].bitcast(I32), 0)
+        nc.gpsimd.memset(w1_planes[0][:, 0:H].bitcast(I32), 0)
+        nc.vector.memset(w1_planes[0][:, H : 2 * H].bitcast(I32), 0)
         for plane in w1_planes[1:] + [w2_plane]:
             nc.vector.memset(plane[:].bitcast(I32), 0)
-        token_planes = []
-        for s in range(K_PASSES):
-            plane = keep.tile([P, T], U8, name=f"xsc{s}", align_bytes=ALIGN)
-            nc.vector.memset(plane[:].bitcast(I32), 0)
-            token_planes.append(plane)
-        token_words = [keep.tile([P, T], U32, name=f"xw{s}", align_bytes=ALIGN) for s in range(K_PASSES)]
 
         result = keep.tile([P, T], F32, name="result", align_bytes=ALIGN)
         nc.vector.memset(result[:], 0.0)
@@ -67,14 +63,15 @@ def tile_moe_pln_mlp_silu_kernel(
         ident = keep.tile([P, P], F32, name="ident", align_bytes=ALIGN)
         make_identity(nc, ident[:])
 
-        raw = [keep.tile([P, 4, T], F32, name=f"raw{s}", align_bytes=ALIGN) for s in range(K_PASSES)]
+        raw = {}
         w1 = {}
         w2 = keep.tile([P, E * H_PASSES, 2 * N], U8, name="w2", align_bytes=ALIGN)
         gates = keep.tile([P, E * C], F32, name="gates", align_bytes=ALIGN)
 
-        def load_x(s, d0, d1):
+        def load_x(s, u):
             rows = xT[PASS * s : PASS * (s + 1), :].rearrange("(p d) w -> p d w", d=4)
-            nc.sync.dma_start(out=raw[s][:, d0:d1, :], in_=rows[:, d0:d1, :])
+            raw[s, u] = keep.tile([P, 2, T], F32, name=f"raw{s}{u}", align_bytes=ALIGN)
+            nc.sync.dma_start(out=raw[s, u][:], in_=rows[:, 2 * u : 2 * u + 2, :])
 
         def load_scales(plane, rows):
             for r in range(4):
@@ -88,91 +85,73 @@ def tile_moe_pln_mlp_silu_kernel(
             nc.sync.dma_start(out=words[:].bitcast(I32), in_=w1_words[slab // K_PASSES, slab % K_PASSES].bitcast(I32))
             w1[slab] = words
 
-        load_x(0, 0, 4)
+        load_x(0, 0)
         nc.sync.dma_start(offsets[:], offs)
-        load_x(1, 0, 4)
-        load_x(LAST, 0, 2)
+        for s, u in ((0, 1), (1, 0), (1, 1), (LAST, 0)):
+            load_x(s, u)
         w1_rows = w1_scales.rearrange("e s q i -> (e s) q i")
-        for r in range(SLABS // RUN):
-            if r == SLABS // RUN - 1:
-                load_scales(w2_plane, w2_scales.rearrange("e s q i -> (e s) q i"))
-            load_scales(w1_planes[r], w1_rows[r * RUN : (r + 1) * RUN])
-            for slab in range(r * RUN, (r + 1) * RUN):
-                load_slab(slab)
-                if slab == 0:
-                    load_x(LAST, 2, 4)
+        load_scales(w1_planes[0], w1_rows[RUNS[0]])
+        load_slab(0)
+        load_x(LAST, 1)
+        load_slab(K_PASSES)
+        load_scales(w1_planes[1], w1_rows[RUNS[1]])
+        load_slab(1)
+        load_scales(w1_planes[2], w1_rows[RUNS[2]])
+        for slab in (2, 4, 5):
+            load_slab(slab)
+        load_scales(w2_plane, w2_scales.rearrange("e s q i -> (e s) q i"))
         nc.sync.dma_start(
             out=w2[:].rearrange("p e b -> p (e b)").bitcast(I32).rearrange("p (e b) -> p e b", e=E * H_PASSES),
             in_=w2_words.bitcast(I32).rearrange("e s p b -> p (e s) b"),
         )
         nc.sync.dma_start(out=gates[:], in_=gate)
 
-        def bank(group, g, name):
-            return psum.tile([P, PASS], F32, name=f"{name}{group}_{g}", tag=f"bank{H_PASSES * group + g}")
+        def bank(number, name):
+            return psum.tile([P, PASS], F32, name=f"{name}{number}", tag=f"bank{number}")
 
-        acc = {(group, g): bank(group, g, "acc") for group in range(GROUPS) for g in range(H_PASSES)}
+        acc = {(group, g): bank(H_PASSES * group + g, "acc") for group in range(GROUPS) for g in range(H_PASSES)}
 
-        def scalar_round(dst, src):
-            nc.scalar.activation(dst, src, COPY)
+        pairs_of, picked, slot_words, slot_planes = {}, {}, {}, {}
 
-        def round_rows(rounded, s, t0, t1, copy):
-            src = raw[s][:, :, t0:t1].rearrange("p d (c i) -> p c d i", i=4)
-            copy(rounded[:, t0:t1, :].rearrange("p (c i) d -> p c d i", i=4), src)
+        def round_pair(s, u):
+            rounded = keep.tile([P, T, 2], BF16, name=f"xb{s}{u}", align_bytes=ALIGN)
+            share = SCALAR_TOKENS.get((s, u), T)
+            src = raw[s, u][:].rearrange("p d w -> p w d")
+            nc.scalar.activation(rounded[:, 0:share, :], src[:, 0:share, :], COPY)
+            if share < T:
+                nc.vector.tensor_copy(rounded[:, share:T, :], src[:, share:T, :])
+            pairs_of[s, u] = rounded[:].rearrange("p w d -> p (w d)").bitcast(U32)
 
-        def round_pair(rounded, s, u, t0, t1, copy):
-            src = raw[s][:, 2 * u : 2 * u + 2, t0:t1].rearrange("p d w -> p w d")
-            copy(rounded[:, t0:t1, 2 * u : 2 * u + 2], src)
+        def gather(s, u, group, groups, pool=keep):
+            if (s, group) not in picked:
+                name = "late" if pool is late else f"xg{s}{group}"
+                picked[s, group] = pool.tile([P, groups * P, 4], BF16, name=name, align_bytes=ALIGN)
+            words = picked[s, group][:].rearrange("p j d -> p (j d)").bitcast(U32).rearrange("p (j u) -> p j u", u=2)
+            nc.vector.tensor_copy(words[:, :, u], pairs_of[s, u].indirect(entries(group * P, groups * P)))
 
-        def quantise_tokens(s):
-            if s == LAST:
-                rounded = reused.tile([P, T, 4], BF16, name=f"xb{s}", align_bytes=ALIGN, offset=0)
-            else:
-                rounded = keep.tile([P, T, 4], BF16, name=f"xb{s}", align_bytes=ALIGN)
-            share = SCALAR_TOKENS[s]
-            if s == LAST:
-                round_pair(rounded, s, 0, 0, T, scalar_round)
-                round_pair(rounded, s, 1, 0, share, scalar_round)
-                round_pair(rounded, s, 1, WIDE, T, nc.vector.tensor_copy)
-                round_pair(rounded, s, 1, share, WIDE, nc.vector.tensor_copy)
-            else:
-                round_rows(rounded, s, 0, share, scalar_round)
-                round_rows(rounded, s, WIDE, T, nc.vector.tensor_copy)
-                round_rows(rounded, s, share, WIDE, nc.vector.tensor_copy)
-            for t0, t1 in ((WIDE, T), (0, WIDE)):
-                nc.vector.quantize_mx(
-                    out=token_words[s][:, t0:t1].bitcast(FP8X4),
-                    scales=token_planes[s][:, t0:t1],
-                    in_=rounded[:, t0:t1, :].rearrange("p w d -> p (w d)"),
-                )
+        def quantise(s, group, groups):
+            words = keep.tile([P, groups * P], U32, name=f"xw{s}{group}", align_bytes=ALIGN)
+            planes = keep.tile([P, groups * P], U8, name=f"xs{s}{group}", align_bytes=ALIGN)
+            nc.vector.quantize_mx(
+                out=words[:].bitcast(FP8X4),
+                scales=planes[:],
+                in_=picked[s, group][:].rearrange("p j d -> p (j d)"),
+            )
+            for c in range(groups):
+                slot_words[s, group + c] = words[:, c * P : (c + 1) * P]
+                slot_planes[s, group + c] = planes[:, c * P : (c + 1) * P]
 
-        slot_words, slot_planes = {}, {}
+        hidden, turned, values, codes, sums, staged = {}, {}, {}, {}, {}, {}
 
-        def gather(s, slot, count, held=False):
-            if held:
-                place = HELD_BYTES * (2 * ((slot - C) // P) + s)
-                words = reused.tile([P, count], U32, name=f"gw{s}_{slot}", align_bytes=ALIGN, offset=place)
-                planes = reused.tile([P, count], U8, name=f"gs{s}_{slot}", align_bytes=ALIGN, offset=place + 4 * count)
-            else:
-                words = keep.tile([P, count], U32, name=f"gw{s}_{slot}", align_bytes=ALIGN)
-                planes = keep.tile([P, count], U8, name=f"gs{s}_{slot}", align_bytes=ALIGN)
-            nc.vector.tensor_copy(words[:], token_words[s][:].indirect(entries(slot, count)))
-            nc.vector.tensor_copy(planes[:], token_planes[s][:].indirect(entries(slot, count)))
-            for c0 in range(0, count, P):
-                slot_words[s, (slot + c0) // P] = words[:, c0 : c0 + P]
-                slot_planes[s, (slot + c0) // P] = planes[:, c0 : c0 + P]
-
-        hidden, turned, sums, staged = {}, {}, {}, {}
-
-        def first_product(group, s):
+        def first_product(group, s, halves=range(H_PASSES)):
             slab = (group * P // C) * K_PASSES + s
-            for g in range(H_PASSES):
-                column = slab % RUN * H + g * PASS
+            for g in halves:
                 nc.tensor.matmul_mx(
                     out=acc[group, g][:],
                     lhsT=slot_words[s, group].bitcast(FP8X4),
                     lhsT_scale=slot_planes[s, group],
                     rhs=w1[slab][:, 2 * g * PASS : 2 * (g + 1) * PASS].bitcast(FP4X4),
-                    rhs_scale=w1_planes[slab // RUN][:, column : column + PASS],
+                    rhs_scale=slab_plane[slab][:, g * PASS : (g + 1) * PASS],
                     start=(s == 0),
                     stop=(s == LAST),
                 )
@@ -188,31 +167,45 @@ def tile_moe_pln_mlp_silu_kernel(
                     SILU,
                 )
 
-        def turn(group):
-            turned[group] = []
-            for g in range(H_PASSES):
-                pairs = bank(group, g, "tp")[:, 0 : 2 * P]
-                for u in range(2):
-                    run = slice(u * P, (u + 1) * P)
-                    nc.tensor.transpose(pairs[:, run], hidden[group][g][:].bitcast(F32)[:, run], ident[:])
-                turned[group].append(pairs)
+        def turn(group, together=False):
+            if together:
+                whole = bank(H_PASSES * group, "tp")
+                pieces = [(0, H_PASSES, whole[:])]
+            else:
+                pieces = [(g, 1, bank(H_PASSES * group + g, "tp")[:, 0 : 2 * P]) for g in range(H_PASSES)]
+            for g0, count, pairs in pieces:
+                for n in range(2 * count):
+                    run = slice(n % 2 * P, (n % 2 + 1) * P)
+                    nc.tensor.transpose(
+                        pairs[:, n * P : (n + 1) * P], hidden[group][g0 + n // 2][:].bitcast(F32)[:, run], ident[:]
+                    )
+            turned[group] = pieces
 
-        def second_product(group):
-            sums[group] = bank(group, 0, "y")
-            values = keep.tile([P, H], BF16, name=f"hb{group}", align_bytes=ALIGN)
+        def interleave(group, copy):
+            values[group] = keep.tile([P, H], BF16, name=f"hb{group}", align_bytes=ALIGN)
+            for g0, count, pairs in turned[group]:
+                copy(
+                    values[group][:, g0 * PASS : (g0 + count) * PASS]
+                    .bitcast(F32)
+                    .rearrange("p (g r u) -> p g r u", g=count, u=2),
+                    pairs.rearrange("p (g u r) -> p g r u", g=count, u=2),
+                )
+
+        def quantise_hidden(group):
             words = keep.tile([P, H_PASSES * P], U32, name=f"hw{group}", align_bytes=ALIGN)
             planes = keep.tile([P, H_PASSES * P], U8, name=f"hc{group}", align_bytes=ALIGN)
-            for g in range(H_PASSES):
-                nc.scalar.copy(
-                    values[:, g * PASS : (g + 1) * PASS].bitcast(F32).rearrange("p (r u) -> p r u", u=2),
-                    turned[group][g].rearrange("p (u r) -> p r u", u=2),
-                )
-            for g in range(H_PASSES):
+            for g0, count, pairs in turned[group]:
                 nc.vector.quantize_mx(
-                    out=words[:, g * P : (g + 1) * P].bitcast(FP8X4),
-                    scales=planes[:, g * P : (g + 1) * P],
-                    in_=values[:, g * PASS : (g + 1) * PASS],
+                    out=words[:, g0 * P : (g0 + count) * P].bitcast(FP8X4),
+                    scales=planes[:, g0 * P : (g0 + count) * P],
+                    in_=values[group][:, g0 * PASS : (g0 + count) * PASS],
                 )
+            codes[group] = (words, planes)
+
+        def second_product(group, number):
+            sums[group] = bank(number, "y")
+            words, planes = codes[group]
+            for g in range(H_PASSES):
                 row = (group * P // C) * H_PASSES + g
                 nc.tensor.matmul_mx(
                     out=sums[group][:, 0:P],
@@ -228,47 +221,79 @@ def tile_moe_pln_mlp_silu_kernel(
             staged[group] = keep.tile([P, P], F32, name=f"yt{group}", align_bytes=ALIGN)
             copy(staged[group][:], sums[group][:, 0:P])
 
-        for s in range(K_PASSES):
-            quantise_tokens(s)
-
-        for s in range(LAST):
-            gather(s, 0, C)
-        for group in range(2):
-            gather(LAST, group * P, P)
-        gather(0, 2 * P, P)
-        gather(0, 3 * P, P, held=True)
-        for group in range(2, GROUPS):
-            for s in range(1, K_PASSES):
-                gather(s, group * P, P, held=s < LAST)
-
-        for s in range(K_PASSES):
-            for group in range(2):
-                first_product(group, s)
-        for group in range(2):
-            activate(group)
-        for group in range(2, GROUPS):
-            first_product(group, 0)
-        for group in range(2):
-            turn(group)
-        for group in range(2, GROUPS):
-            for s in range(1, K_PASSES):
-                first_product(group, s)
-            activate(group)
-            second_product(group - 2)
-            stage(group - 2, nc.vector.tensor_copy)
-        for group in range(2, GROUPS):
-            turn(group)
-        for group in range(2, GROUPS):
-            second_product(group)
-        for group in range(2, GROUPS):
-            stage(group, nc.scalar.copy)
-
-        for group in range(GROUPS):
+        def scatter(group):
             nc.vector.tensor_tensor(
                 result[:].indirect(entries(group * P, P)),
                 staged[group][:],
                 gates[:, group * P : (group + 1) * P],
                 MULT,
             )
+
+        for u in range(2):
+            round_pair(0, u)
+            for group in (0, 2):
+                gather(0, u, group, 2)
+        for group in (0, 2):
+            quantise(0, group, 2)
+        for u in range(2):
+            round_pair(1, u)
+            gather(1, u, 0, 2)
+            gather(1, u, 2, 1)
+        quantise(1, 0, 2)
+        quantise(1, 2, 1)
+        for u in range(2):
+            round_pair(LAST, u)
+            for group in range(2):
+                gather(LAST, u, group, 1, late)
+        for group in range(2):
+            quantise(LAST, group, 1)
+        for s, group in ((LAST, 2), (1, 3)):
+            for u in range(2):
+                gather(s, u, group, 1, late)
+        quantise(LAST, 2, 1)
+        quantise(1, 3, 1)
+        for u in range(2):
+            gather(LAST, u, 3, 1, late)
+        quantise(LAST, 3, 1)
+
+        for group in range(GROUPS):
+            first_product(group, 0)
+        for group in range(2):
+            first_product(group, 1)
+        for group in range(2):
+            first_product(group, LAST)
+            activate(group)
+        first_product(2, 1)
+        turn(0)
+        interleave(0, nc.scalar.copy)
+        first_product(2, LAST)
+        quantise_hidden(0)
+        activate(2)
+        turn(1, together=True)
+        interleave(1, nc.vector.tensor_copy)
+        for g in range(H_PASSES):
+            for s in range(1, K_PASSES):
+                first_product(3, s, (g,))
+            if g == 0:
+                second_product(0, 0)
+        activate(3)
+        stage(0, nc.vector.tensor_copy)
+        quantise_hidden(1)
+        scatter(0)
+        turn(2)
+        second_product(1, 3)
+        interleave(2, nc.scalar.copy)
+        turn(3)
+        stage(1, nc.scalar.copy)
+        quantise_hidden(2)
+        interleave(3, nc.scalar.copy)
+        scatter(1)
+        second_product(2, 4)
+        quantise_hidden(3)
+        stage(2, nc.scalar.copy)
+        second_product(3, 6)
+        scatter(2)
+        stage(3, nc.scalar.copy)
+        scatter(3)
 
         nc.sync.dma_start(out=out, in_=result[:])

@@ -27,7 +27,7 @@ LIST_ROWS = 16
 ALIGN = 256
 FLOPS = 2 * E * C * (K * H + H * N)
 
-SCALAR_TOKENS = {(0, 0): 224, (0, 1): 384, (K_PASSES - 1, 1): 320}
+SCALAR_TOKENS = {(0, 0): 224, (0, 1): 448, (K_PASSES - 1, 1): 384}
 RUNS = (slice(0, SLABS, K_PASSES), slice(1, K_PASSES), slice(K_PASSES + 1, SLABS))
 
 
@@ -93,8 +93,8 @@ def tile_moe_pln_mlp_silu_kernel(
         load_scales(w1_planes[0], w1_rows[RUNS[0]])
         load_slab(0)
         load_x(LAST, 1)
-        load_slab(K_PASSES)
         load_scales(w1_planes[1], w1_rows[RUNS[1]])
+        load_slab(K_PASSES)
         load_slab(1)
         load_scales(w1_planes[2], w1_rows[RUNS[2]])
         for slab in (2, 4, 5):
@@ -111,7 +111,7 @@ def tile_moe_pln_mlp_silu_kernel(
 
         acc = {(group, g): bank(H_PASSES * group + g, "acc") for group in range(GROUPS) for g in range(H_PASSES)}
 
-        pairs_of, picked, slot_words, slot_planes = {}, {}, {}, {}
+        pairs_of, apart, picked, slot_words, slot_planes = {}, {}, {}, {}, {}
 
         def round_pair(s, u):
             rounded = keep.tile([P, T, 2], BF16, name=f"xb{s}{u}", align_bytes=ALIGN)
@@ -122,12 +122,23 @@ def tile_moe_pln_mlp_silu_kernel(
                 nc.vector.tensor_copy(rounded[:, share:T, :], src[:, share:T, :])
             pairs_of[s, u] = rounded[:].rearrange("p w d -> p (w d)").bitcast(U32)
 
-        def gather(s, u, group, groups, pool=keep):
+        def gather_apart(s, u, group, groups):
+            if (s, group) not in apart:
+                apart[s, group] = keep.tile([P, 2, groups * P], U32, name=f"xa{s}{group}", align_bytes=ALIGN)
+            nc.vector.tensor_copy(apart[s, group][:, u, :], pairs_of[s, u].indirect(entries(group * P, groups * P)))
+
+        def weave(s, group, groups):
+            picked[s, group] = keep.tile([P, groups * P, 4], BF16, name=f"xg{s}{group}", align_bytes=ALIGN)
+            nc.vector.tensor_copy(
+                picked[s, group][:].bitcast(I32), apart[s, group][:].bitcast(I32).rearrange("p u j -> p j u")
+            )
+
+        def gather_woven(s, u, group):
             if (s, group) not in picked:
-                name = "late" if pool is late else f"xg{s}{group}"
-                picked[s, group] = pool.tile([P, groups * P, 4], BF16, name=name, align_bytes=ALIGN)
-            words = picked[s, group][:].rearrange("p j d -> p (j d)").bitcast(U32).rearrange("p (j u) -> p j u", u=2)
-            nc.vector.tensor_copy(words[:, :, u], pairs_of[s, u].indirect(entries(group * P, groups * P)))
+                picked[s, group] = late.tile([P, P, 4], BF16, name="late", align_bytes=ALIGN)
+            nc.vector.tensor_copy(
+                picked[s, group][:].bitcast(U32)[:, :, u], pairs_of[s, u].indirect(entries(group * P, P))
+            )
 
         def quantise(s, group, groups):
             words = keep.tile([P, groups * P], U32, name=f"xw{s}{group}", align_bytes=ALIGN)
@@ -229,31 +240,28 @@ def tile_moe_pln_mlp_silu_kernel(
                 MULT,
             )
 
-        for u in range(2):
-            round_pair(0, u)
-            for group in (0, 2):
-                gather(0, u, group, 2)
-        for group in (0, 2):
-            quantise(0, group, 2)
-        for u in range(2):
-            round_pair(1, u)
-            gather(1, u, 0, 2)
-            gather(1, u, 2, 1)
-        quantise(1, 0, 2)
-        quantise(1, 2, 1)
+        for s, spans in ((0, ((0, 2), (2, 2))), (1, ((0, 2), (2, 1)))):
+            for u in range(2):
+                round_pair(s, u)
+                for group, groups in spans:
+                    gather_apart(s, u, group, groups)
+            for group, groups in spans:
+                weave(s, group, groups)
+            for group, groups in spans:
+                quantise(s, group, groups)
         for u in range(2):
             round_pair(LAST, u)
             for group in range(2):
-                gather(LAST, u, group, 1, late)
+                gather_woven(LAST, u, group)
         for group in range(2):
             quantise(LAST, group, 1)
         for s, group in ((LAST, 2), (1, 3)):
             for u in range(2):
-                gather(s, u, group, 1, late)
+                gather_woven(s, u, group)
         quantise(LAST, 2, 1)
         quantise(1, 3, 1)
         for u in range(2):
-            gather(LAST, u, 3, 1, late)
+            gather_woven(LAST, u, 3)
         quantise(LAST, 3, 1)
 
         for group in range(GROUPS):

@@ -27,8 +27,10 @@ LIST_ROWS = 16
 ALIGN = 256
 FLOPS = 2 * E * C * (K * H + H * N)
 
-SCALAR_TOKENS = {(0, 0): 224, (0, 1): 448, (K_PASSES - 1, 1): 384}
+SCALAR_TOKENS = {(0, 0): 224, (0, 1): 448, (LAST, 1): 384}
 RUNS = (slice(0, SLABS, K_PASSES), slice(1, K_PASSES), slice(K_PASSES + 1, SLABS))
+RUN = 2
+VECTOR_GROUP = 1
 
 
 def tile_moe_pln_mlp_silu_kernel(
@@ -46,14 +48,14 @@ def tile_moe_pln_mlp_silu_kernel(
         def entries(slot, count):
             return offsets[:, slot // LIST_ROWS : (slot + count) // LIST_ROWS]
 
-        w1_planes = [keep.tile([P, 2 * H], U8, name=f"w1s{r}", align_bytes=ALIGN) for r in range(len(RUNS))]
+        w1_planes = [keep.tile([P, RUN * H], U8, name=f"w1s{r}", align_bytes=ALIGN) for r in range(len(RUNS))]
         slab_plane = {}
         for plane, run in zip(w1_planes, RUNS):
             for n, slab in enumerate(range(SLABS)[run]):
                 slab_plane[slab] = plane[:, n * H : (n + 1) * H]
         w2_plane = keep.tile([P, E * H_PASSES * N], U8, name="w2s", align_bytes=ALIGN)
         nc.gpsimd.memset(w1_planes[0][:, 0:H].bitcast(I32), 0)
-        nc.vector.memset(w1_planes[0][:, H : 2 * H].bitcast(I32), 0)
+        nc.vector.memset(w1_planes[0][:, H : RUN * H].bitcast(I32), 0)
         for plane in w1_planes[1:] + [w2_plane]:
             nc.vector.memset(plane[:].bitcast(I32), 0)
 
@@ -97,7 +99,8 @@ def tile_moe_pln_mlp_silu_kernel(
         load_slab(K_PASSES)
         load_slab(1)
         load_scales(w1_planes[2], w1_rows[RUNS[2]])
-        for slab in (2, 4, 5):
+        load_slab(LAST)
+        for slab in range(K_PASSES + 1, SLABS):
             load_slab(slab)
         load_scales(w2_plane, w2_scales.rearrange("e s q i -> (e s) q i"))
         nc.sync.dma_start(
@@ -178,10 +181,9 @@ def tile_moe_pln_mlp_silu_kernel(
                     SILU,
                 )
 
-        def turn(group, together=False):
-            if together:
-                whole = bank(H_PASSES * group, "tp")
-                pieces = [(0, H_PASSES, whole[:])]
+        def turn(group):
+            if group == VECTOR_GROUP:
+                pieces = [(0, H_PASSES, bank(H_PASSES * group, "tp")[:])]
             else:
                 pieces = [(g, 1, bank(H_PASSES * group + g, "tp")[:, 0 : 2 * P]) for g in range(H_PASSES)]
             for g0, count, pairs in pieces:
@@ -192,7 +194,8 @@ def tile_moe_pln_mlp_silu_kernel(
                     )
             turned[group] = pieces
 
-        def interleave(group, copy):
+        def interleave(group):
+            copy = nc.vector.tensor_copy if group == VECTOR_GROUP else nc.scalar.copy
             values[group] = keep.tile([P, H], BF16, name=f"hb{group}", align_bytes=ALIGN)
             for g0, count, pairs in turned[group]:
                 copy(
@@ -213,8 +216,8 @@ def tile_moe_pln_mlp_silu_kernel(
                 )
             codes[group] = (words, planes)
 
-        def second_product(group, number):
-            sums[group] = bank(number, "y")
+        def second_product(group):
+            sums[group] = bank(H_PASSES * group + (group == VECTOR_GROUP), "y")
             words, planes = codes[group]
             for g in range(H_PASSES):
                 row = (group * P // C) * H_PASSES + g
@@ -228,7 +231,8 @@ def tile_moe_pln_mlp_silu_kernel(
                     stop=(g == H_PASSES - 1),
                 )
 
-        def stage(group, copy):
+        def stage(group):
+            copy = nc.vector.tensor_copy if group == 0 else nc.scalar.copy
             staged[group] = keep.tile([P, P], F32, name=f"yt{group}", align_bytes=ALIGN)
             copy(staged[group][:], sums[group][:, 0:P])
 
@@ -255,14 +259,12 @@ def tile_moe_pln_mlp_silu_kernel(
                 gather_woven(LAST, u, group)
         for group in range(2):
             quantise(LAST, group, 1)
-        for s, group in ((LAST, 2), (1, 3)):
-            for u in range(2):
-                gather_woven(s, u, group)
-        quantise(LAST, 2, 1)
-        quantise(1, 3, 1)
-        for u in range(2):
-            gather_woven(LAST, u, 3)
-        quantise(LAST, 3, 1)
+        for batch in (((LAST, 2), (1, 3)), ((LAST, 3),)):
+            for s, group in batch:
+                for u in range(2):
+                    gather_woven(s, u, group)
+            for s, group in batch:
+                quantise(s, group, 1)
 
         for group in range(GROUPS):
             first_product(group, 0)
@@ -273,35 +275,26 @@ def tile_moe_pln_mlp_silu_kernel(
             activate(group)
         first_product(2, 1)
         turn(0)
-        interleave(0, nc.scalar.copy)
+        interleave(0)
         first_product(2, LAST)
         quantise_hidden(0)
         activate(2)
-        turn(1, together=True)
-        interleave(1, nc.vector.tensor_copy)
-        for g in range(H_PASSES):
-            for s in range(1, K_PASSES):
-                first_product(3, s, (g,))
-            if g == 0:
-                second_product(0, 0)
-        activate(3)
-        stage(0, nc.vector.tensor_copy)
-        quantise_hidden(1)
-        scatter(0)
-        turn(2)
-        second_product(1, 3)
-        interleave(2, nc.scalar.copy)
-        turn(3)
-        stage(1, nc.scalar.copy)
-        quantise_hidden(2)
-        interleave(3, nc.scalar.copy)
-        scatter(1)
-        second_product(2, 4)
-        quantise_hidden(3)
-        stage(2, nc.scalar.copy)
-        second_product(3, 6)
-        scatter(2)
-        stage(3, nc.scalar.copy)
-        scatter(3)
+
+        for group in range(1, GROUPS + 1):
+            if group < GROUPS:
+                turn(group)
+                interleave(group)
+            if group == 1:
+                for s in range(1, K_PASSES):
+                    first_product(3, s, (0,))
+            second_product(group - 1)
+            if group == 1:
+                for s in range(1, K_PASSES):
+                    first_product(3, s, (1,))
+                activate(3)
+            stage(group - 1)
+            if group < GROUPS:
+                quantise_hidden(group)
+            scatter(group - 1)
 
         nc.sync.dma_start(out=out, in_=result[:])

@@ -22,15 +22,16 @@ K_PASSES = K // PASS
 H_PASSES = H // PASS
 LAST = K_PASSES - 1
 GROUPS = E * C // P
+PER_EXPERT = C // P
 SLABS = E * K_PASSES
 LIST_ROWS = 16
 ALIGN = 256
 FLOPS = 2 * E * C * (K * H + H * N)
 
-SCALAR_TOKENS = {(0, 0): 224, (0, 1): 448, (LAST, 1): 384}
+SCALAR_TOKENS = {(0, 0): 224, (0, 1): 448, (LAST, 1): 320}
 RUNS = (slice(0, SLABS, K_PASSES), slice(1, K_PASSES), slice(K_PASSES + 1, SLABS))
 RUN = 2
-VECTOR_GROUP = 1
+SUMS_BANK = (0, 1, 3, 2)
 
 
 def tile_moe_pln_mlp_silu_kernel(
@@ -48,16 +49,28 @@ def tile_moe_pln_mlp_silu_kernel(
         def entries(slot, count):
             return offsets[:, slot // LIST_ROWS : (slot + count) // LIST_ROWS]
 
+        warm = keep.tile([P, 2], F32, name="warm", align_bytes=ALIGN)
+        nc.vector.memset(warm[:, 0:1], 0.0)
+        nc.scalar.activation(warm[:, 1:2], warm[:, 0:1], SILU)
+
         w1_planes = [keep.tile([P, RUN * H], U8, name=f"w1s{r}", align_bytes=ALIGN) for r in range(len(RUNS))]
         slab_plane = {}
         for plane, run in zip(w1_planes, RUNS):
             for n, slab in enumerate(range(SLABS)[run]):
                 slab_plane[slab] = plane[:, n * H : (n + 1) * H]
         w2_plane = keep.tile([P, E * H_PASSES * N], U8, name="w2s", align_bytes=ALIGN)
-        nc.gpsimd.memset(w1_planes[0][:, 0:H].bitcast(I32), 0)
-        nc.vector.memset(w1_planes[0][:, H : RUN * H].bitcast(I32), 0)
-        for plane in w1_planes[1:] + [w2_plane]:
+        for plane in w1_planes:
             nc.vector.memset(plane[:].bitcast(I32), 0)
+        nc.gpsimd.memset(w2_plane[:].bitcast(I32), 0)
+
+        def load_scales(queue, plane, rows):
+            for r in range(4):
+                queue.dma_start(
+                    out=plane[r:P:32, :].bitcast(I32).rearrange("q (s i) -> q s i", s=rows.shape[0]),
+                    in_=rows[:, r:16:4, :].bitcast(I32).rearrange("s q i -> q s i"),
+                )
+
+        load_scales(nc.gpsimd, w2_plane, w2_scales.rearrange("e s q i -> (e s) q i"))
 
         result = keep.tile([P, T], F32, name="result", align_bytes=ALIGN)
         nc.vector.memset(result[:], 0.0)
@@ -75,13 +88,6 @@ def tile_moe_pln_mlp_silu_kernel(
             raw[s, u] = keep.tile([P, 2, T], F32, name=f"raw{s}{u}", align_bytes=ALIGN)
             nc.sync.dma_start(out=raw[s, u][:], in_=rows[:, 2 * u : 2 * u + 2, :])
 
-        def load_scales(plane, rows):
-            for r in range(4):
-                nc.sync.dma_start(
-                    out=plane[r:P:32, :].bitcast(I32).rearrange("q (s i) -> q s i", s=rows.shape[0]),
-                    in_=rows[:, r:16:4, :].bitcast(I32).rearrange("s q i -> q s i"),
-                )
-
         def load_slab(slab):
             words = keep.tile([P, 2 * H], U8, name=f"w1_{slab}", align_bytes=ALIGN)
             nc.sync.dma_start(out=words[:].bitcast(I32), in_=w1_words[slab // K_PASSES, slab % K_PASSES].bitcast(I32))
@@ -89,30 +95,31 @@ def tile_moe_pln_mlp_silu_kernel(
 
         load_x(0, 0)
         nc.sync.dma_start(offsets[:], offs)
-        for s, u in ((0, 1), (1, 0), (1, 1), (LAST, 0)):
+        for s, u in ((0, 1), (1, 0), (1, 1)):
             load_x(s, u)
         w1_rows = w1_scales.rearrange("e s q i -> (e s) q i")
-        load_scales(w1_planes[0], w1_rows[RUNS[0]])
+        load_scales(nc.sync, w1_planes[0], w1_rows[RUNS[0]])
         load_slab(0)
-        load_x(LAST, 1)
-        load_scales(w1_planes[1], w1_rows[RUNS[1]])
+        load_x(LAST, 0)
         load_slab(K_PASSES)
+        load_x(LAST, 1)
+        load_scales(nc.sync, w1_planes[1], w1_rows[RUNS[1]])
         load_slab(1)
-        load_scales(w1_planes[2], w1_rows[RUNS[2]])
+        load_scales(nc.sync, w1_planes[2], w1_rows[RUNS[2]])
         load_slab(LAST)
         for slab in range(K_PASSES + 1, SLABS):
             load_slab(slab)
-        load_scales(w2_plane, w2_scales.rearrange("e s q i -> (e s) q i"))
         nc.sync.dma_start(
             out=w2[:].rearrange("p e b -> p (e b)").bitcast(I32).rearrange("p (e b) -> p e b", e=E * H_PASSES),
             in_=w2_words.bitcast(I32).rearrange("e s p b -> p (e s) b"),
         )
         nc.sync.dma_start(out=gates[:], in_=gate)
 
-        def bank(number, name):
+        def bank(group, g, name):
+            number = H_PASSES * group + g
             return psum.tile([P, PASS], F32, name=f"{name}{number}", tag=f"bank{number}")
 
-        acc = {(group, g): bank(H_PASSES * group + g, "acc") for group in range(GROUPS) for g in range(H_PASSES)}
+        acc = {(group, g): bank(group, g, "acc") for group in range(GROUPS) for g in range(H_PASSES)}
 
         pairs_of, apart, picked, slot_words, slot_planes = {}, {}, {}, {}, {}
 
@@ -125,22 +132,23 @@ def tile_moe_pln_mlp_silu_kernel(
                 nc.vector.tensor_copy(rounded[:, share:T, :], src[:, share:T, :])
             pairs_of[s, u] = rounded[:].rearrange("p w d -> p (w d)").bitcast(U32)
 
-        def gather_apart(s, u, group, groups):
-            if (s, group) not in apart:
-                apart[s, group] = keep.tile([P, 2, groups * P], U32, name=f"xa{s}{group}", align_bytes=ALIGN)
-            nc.vector.tensor_copy(apart[s, group][:, u, :], pairs_of[s, u].indirect(entries(group * P, groups * P)))
+        def runs_tile(s, group, groups, pool, name):
+            runs = pool.tile([P, 2, groups * P], U32, name=name, align_bytes=ALIGN)
+            for c in range(groups):
+                apart[s, group + c] = (runs, c * P)
 
-        def weave(s, group, groups):
-            picked[s, group] = keep.tile([P, groups * P, 4], BF16, name=f"xg{s}{group}", align_bytes=ALIGN)
+        def gather(s, u, group, groups):
+            runs, first = apart[s, group]
             nc.vector.tensor_copy(
-                picked[s, group][:].bitcast(I32), apart[s, group][:].bitcast(I32).rearrange("p u j -> p j u")
+                runs[:, u, first : first + groups * P], pairs_of[s, u].indirect(entries(group * P, groups * P))
             )
 
-        def gather_woven(s, u, group):
-            if (s, group) not in picked:
-                picked[s, group] = late.tile([P, P, 4], BF16, name="late", align_bytes=ALIGN)
-            nc.vector.tensor_copy(
-                picked[s, group][:].bitcast(U32)[:, :, u], pairs_of[s, u].indirect(entries(group * P, P))
+        def weave(s, group, groups, pool, name, copy=nc.vector.tensor_copy, word=I32):
+            runs, first = apart[s, group]
+            picked[s, group] = pool.tile([P, groups * P, 4], BF16, name=name, align_bytes=ALIGN)
+            copy(
+                picked[s, group][:].bitcast(word),
+                runs[:, :, first : first + groups * P].bitcast(word).rearrange("p u j -> p j u"),
             )
 
         def quantise(s, group, groups):
@@ -158,7 +166,7 @@ def tile_moe_pln_mlp_silu_kernel(
         hidden, turned, values, codes, sums, staged = {}, {}, {}, {}, {}, {}
 
         def first_product(group, s, halves=range(H_PASSES)):
-            slab = (group * P // C) * K_PASSES + s
+            slab = (group // PER_EXPERT) * K_PASSES + s
             for g in halves:
                 nc.tensor.matmul_mx(
                     out=acc[group, g][:],
@@ -170,73 +178,59 @@ def tile_moe_pln_mlp_silu_kernel(
                     stop=(s == LAST),
                 )
 
-        def activate(group):
-            hidden[group] = [
-                keep.tile([P, PASS], BF16, name=f"hs{group}_{g}", align_bytes=ALIGN) for g in range(H_PASSES)
-            ]
-            for g in range(H_PASSES):
-                nc.scalar.activation(
-                    hidden[group][g][:].rearrange("p (u m d) -> p u m d", u=2, d=2),
-                    acc[group, g][:].rearrange("p (m u d) -> p u m d", u=2, d=2),
-                    SILU,
-                )
+        def activate(group, g):
+            hidden[group, g] = keep.tile([P, PASS], BF16, name=f"hs{group}_{g}", align_bytes=ALIGN)
+            nc.scalar.activation(
+                hidden[group, g][:].rearrange("p (u m d) -> p u m d", u=2, d=2),
+                acc[group, g][:].rearrange("p (m u d) -> p u m d", u=2, d=2),
+                SILU,
+            )
 
-        def turn(group):
-            if group == VECTOR_GROUP:
-                pieces = [(0, H_PASSES, bank(H_PASSES * group, "tp")[:])]
-            else:
-                pieces = [(g, 1, bank(H_PASSES * group + g, "tp")[:, 0 : 2 * P]) for g in range(H_PASSES)]
-            for g0, count, pairs in pieces:
-                for n in range(2 * count):
-                    run = slice(n % 2 * P, (n % 2 + 1) * P)
-                    nc.tensor.transpose(
-                        pairs[:, n * P : (n + 1) * P], hidden[group][g0 + n // 2][:].bitcast(F32)[:, run], ident[:]
-                    )
-            turned[group] = pieces
+        def turn(group, g):
+            turned[group, g] = bank(group, g, "tp")[:, 0 : 2 * P]
+            for u in range(2):
+                run = slice(u * P, (u + 1) * P)
+                nc.tensor.transpose(turned[group, g][:, run], hidden[group, g][:].bitcast(F32)[:, run], ident[:])
 
-        def interleave(group):
-            copy = nc.vector.tensor_copy if group == VECTOR_GROUP else nc.scalar.copy
-            values[group] = keep.tile([P, H], BF16, name=f"hb{group}", align_bytes=ALIGN)
-            for g0, count, pairs in turned[group]:
-                copy(
-                    values[group][:, g0 * PASS : (g0 + count) * PASS]
-                    .bitcast(F32)
-                    .rearrange("p (g r u) -> p g r u", g=count, u=2),
-                    pairs.rearrange("p (g u r) -> p g r u", g=count, u=2),
-                )
+        def interleave(group, g):
+            copy = nc.vector.tensor_copy if group < PER_EXPERT else nc.scalar.copy
+            values[group, g] = keep.tile([P, PASS], BF16, name=f"hb{group}_{g}", align_bytes=ALIGN)
+            copy(
+                values[group, g][:].bitcast(F32).rearrange("p (r u) -> p r u", u=2),
+                turned[group, g].rearrange("p (u r) -> p r u", u=2),
+            )
 
-        def quantise_hidden(group):
-            words = keep.tile([P, H_PASSES * P], U32, name=f"hw{group}", align_bytes=ALIGN)
-            planes = keep.tile([P, H_PASSES * P], U8, name=f"hc{group}", align_bytes=ALIGN)
-            for g0, count, pairs in turned[group]:
-                nc.vector.quantize_mx(
-                    out=words[:, g0 * P : (g0 + count) * P].bitcast(FP8X4),
-                    scales=planes[:, g0 * P : (g0 + count) * P],
-                    in_=values[group][:, g0 * PASS : (g0 + count) * PASS],
-                )
-            codes[group] = (words, planes)
+        def quantise_hidden(group, g):
+            words = keep.tile([P, P], U32, name=f"hw{group}_{g}", align_bytes=ALIGN)
+            planes = keep.tile([P, P], U8, name=f"hc{group}_{g}", align_bytes=ALIGN)
+            nc.vector.quantize_mx(out=words[:].bitcast(FP8X4), scales=planes[:], in_=values[group, g][:])
+            codes[group, g] = (words, planes)
+
+        def hand_over(group):
+            for step in (turn, interleave, quantise_hidden):
+                for g in range(H_PASSES):
+                    step(group, g)
 
         def second_product(group):
-            sums[group] = bank(H_PASSES * group + (group == VECTOR_GROUP), "y")
-            words, planes = codes[group]
+            sums[group] = bank(SUMS_BANK[group], 0, "y")
             for g in range(H_PASSES):
-                row = (group * P // C) * H_PASSES + g
+                words, planes = codes[group, g]
+                row = (group // PER_EXPERT) * H_PASSES + g
                 nc.tensor.matmul_mx(
                     out=sums[group][:, 0:P],
                     lhsT=w2[:, row, :].bitcast(FP4X4),
                     lhsT_scale=w2_plane[:, row * N : (row + 1) * N],
-                    rhs=words[:, g * P : (g + 1) * P].bitcast(FP8X4),
-                    rhs_scale=planes[:, g * P : (g + 1) * P],
+                    rhs=words[:].bitcast(FP8X4),
+                    rhs_scale=planes[:],
                     start=(g == 0),
                     stop=(g == H_PASSES - 1),
                 )
 
-        def stage(group):
+        def put_back(group):
             copy = nc.vector.tensor_copy if group == 0 else nc.scalar.copy
-            staged[group] = keep.tile([P, P], F32, name=f"yt{group}", align_bytes=ALIGN)
+            name = f"hs{group + 1}_{H_PASSES - 1}"
+            staged[group] = keep.tile([P, P], F32, name=name, align_bytes=ALIGN)
             copy(staged[group][:], sums[group][:, 0:P])
-
-        def scatter(group):
             nc.vector.tensor_tensor(
                 result[:].indirect(entries(group * P, P)),
                 staged[group][:],
@@ -244,57 +238,66 @@ def tile_moe_pln_mlp_silu_kernel(
                 MULT,
             )
 
-        for s, spans in ((0, ((0, 2), (2, 2))), (1, ((0, 2), (2, 1)))):
+        experts = [(e * PER_EXPERT, PER_EXPERT) for e in range(E)]
+        for s in range(LAST):
+            for group, groups in experts:
+                runs_tile(s, group, groups, keep, f"xa{s}{group}")
             for u in range(2):
                 round_pair(s, u)
-                for group, groups in spans:
-                    gather_apart(s, u, group, groups)
-            for group, groups in spans:
-                weave(s, group, groups)
-            for group, groups in spans:
-                quantise(s, group, groups)
-        for u in range(2):
-            round_pair(LAST, u)
-            for group in range(2):
-                gather_woven(LAST, u, group)
-        for group in range(2):
+                for group, groups in experts:
+                    gather(s, u, group, groups)
+            weave(s, 0, PER_EXPERT, keep, f"xg{s}")
+            quantise(s, 0, PER_EXPERT)
+        weave(0, PER_EXPERT, PER_EXPERT, keep, "raw11", nc.scalar.copy, U32)
+        quantise(0, PER_EXPERT, PER_EXPERT)
+        runs_tile(LAST, 0, PER_EXPERT, keep, "xa_last")
+        round_pair(LAST, 0)
+        gather(LAST, 0, 0, PER_EXPERT)
+        round_pair(LAST, 1)
+        weave(1, PER_EXPERT, PER_EXPERT, keep, "raw21", nc.scalar.copy, U32)
+        for group in range(PER_EXPERT):
+            gather(LAST, 1, group, 1)
+        for group in range(PER_EXPERT):
+            weave(LAST, group, 1, late, "late", nc.scalar.copy, U32)
+        for group in range(PER_EXPERT):
             quantise(LAST, group, 1)
-        for batch in (((LAST, 2), (1, 3)), ((LAST, 3),)):
-            for s, group in batch:
-                for u in range(2):
-                    gather_woven(s, u, group)
-            for s, group in batch:
-                quantise(s, group, 1)
+        quantise(1, PER_EXPERT, PER_EXPERT)
+        for group in range(PER_EXPERT, GROUPS):
+            runs_tile(LAST, group, 1, late, "late")
+            for u in range(2):
+                gather(LAST, u, group, 1)
+            weave(LAST, group, 1, keep, f"xg_last{group}")
+            quantise(LAST, group, 1)
 
         for group in range(GROUPS):
             first_product(group, 0)
-        for group in range(2):
+        for group in range(PER_EXPERT):
             first_product(group, 1)
-        for group in range(2):
+        for group in range(PER_EXPERT):
             first_product(group, LAST)
-            activate(group)
+            for g in range(H_PASSES):
+                activate(group, g)
         first_product(2, 1)
-        turn(0)
-        interleave(0)
+        hand_over(0)
         first_product(2, LAST)
-        quantise_hidden(0)
-        activate(2)
-
-        for group in range(1, GROUPS + 1):
-            if group < GROUPS:
-                turn(group)
-                interleave(group)
-            if group == 1:
-                for s in range(1, K_PASSES):
-                    first_product(3, s, (0,))
-            second_product(group - 1)
-            if group == 1:
-                for s in range(1, K_PASSES):
-                    first_product(3, s, (1,))
-                activate(3)
-            stage(group - 1)
-            if group < GROUPS:
-                quantise_hidden(group)
-            scatter(group - 1)
+        for g in range(H_PASSES):
+            activate(2, g)
+        hand_over(1)
+        second_product(0)
+        put_back(0)
+        for s in range(1, K_PASSES):
+            first_product(3, s, (0,))
+        activate(3, 0)
+        hand_over(2)
+        second_product(1)
+        put_back(1)
+        for s in range(1, K_PASSES):
+            first_product(3, s, (1,))
+        activate(3, 1)
+        hand_over(3)
+        second_product(2)
+        put_back(2)
+        second_product(3)
+        put_back(3)
 
         nc.sync.dma_start(out=out, in_=result[:])

@@ -59,18 +59,8 @@ def tile_moe_pln_mlp_silu_kernel(
             for n, slab in enumerate(range(SLABS)[run]):
                 slab_plane[slab] = plane[:, n * H : (n + 1) * H]
         w2_plane = keep.tile([P, E * H_PASSES * N], U8, name="w2s", align_bytes=ALIGN)
-        for plane in w1_planes:
+        for plane in w1_planes + [w2_plane]:
             nc.vector.memset(plane[:].bitcast(I32), 0)
-        nc.gpsimd.memset(w2_plane[:].bitcast(I32), 0)
-
-        def load_scales(queue, plane, rows):
-            for r in range(4):
-                queue.dma_start(
-                    out=plane[r:P:32, :].bitcast(I32).rearrange("q (s i) -> q s i", s=rows.shape[0]),
-                    in_=rows[:, r:16:4, :].bitcast(I32).rearrange("s q i -> q s i"),
-                )
-
-        load_scales(nc.gpsimd, w2_plane, w2_scales.rearrange("e s q i -> (e s) q i"))
 
         result = keep.tile([P, T], F32, name="result", align_bytes=ALIGN)
         nc.vector.memset(result[:], 0.0)
@@ -88,6 +78,13 @@ def tile_moe_pln_mlp_silu_kernel(
             raw[s, u] = keep.tile([P, 2, T], F32, name=f"raw{s}{u}", align_bytes=ALIGN)
             nc.sync.dma_start(out=raw[s, u][:], in_=rows[:, 2 * u : 2 * u + 2, :])
 
+        def load_scales(plane, rows):
+            for r in range(4):
+                nc.sync.dma_start(
+                    out=plane[r:P:32, :].bitcast(I32).rearrange("q (s i) -> q s i", s=rows.shape[0]),
+                    in_=rows[:, r:16:4, :].bitcast(I32).rearrange("s q i -> q s i"),
+                )
+
         def load_slab(slab):
             words = keep.tile([P, 2 * H], U8, name=f"w1_{slab}", align_bytes=ALIGN)
             nc.sync.dma_start(out=words[:].bitcast(I32), in_=w1_words[slab // K_PASSES, slab % K_PASSES].bitcast(I32))
@@ -98,14 +95,15 @@ def tile_moe_pln_mlp_silu_kernel(
         for s, u in ((0, 1), (1, 0), (1, 1)):
             load_x(s, u)
         w1_rows = w1_scales.rearrange("e s q i -> (e s) q i")
-        load_scales(nc.sync, w1_planes[0], w1_rows[RUNS[0]])
+        load_scales(w1_planes[0], w1_rows[RUNS[0]])
         load_slab(0)
         load_x(LAST, 0)
         load_slab(K_PASSES)
+        load_scales(w2_plane, w2_scales.rearrange("e s q i -> (e s) q i"))
         load_x(LAST, 1)
-        load_scales(nc.sync, w1_planes[1], w1_rows[RUNS[1]])
+        load_scales(w1_planes[1], w1_rows[RUNS[1]])
         load_slab(1)
-        load_scales(nc.sync, w1_planes[2], w1_rows[RUNS[2]])
+        load_scales(w1_planes[2], w1_rows[RUNS[2]])
         load_slab(LAST)
         for slab in range(K_PASSES + 1, SLABS):
             load_slab(slab)

@@ -28,10 +28,9 @@ LIST_ROWS = 16
 ALIGN = 256
 FLOPS = 2 * E * C * (K * H + H * N)
 
-SCALAR_TOKENS = {(0, 0): 224, (0, 1): 448, (LAST, 1): 320}
+SCALAR_TOKENS = {(0, 0): 224, (0, 1): 448, (LAST, 1): 384}
 RUNS = (slice(0, SLABS, K_PASSES), slice(1, K_PASSES), slice(K_PASSES + 1, SLABS))
 RUN = 2
-SUMS_BANK = (0, 1, 3, 2)
 
 
 def tile_moe_pln_mlp_silu_kernel(
@@ -41,6 +40,7 @@ def tile_moe_pln_mlp_silu_kernel(
     with ExitStack() as ctx:
         lists = ctx.enter_context(tc.tile_pool(name="lists", bufs=1))
         keep = ctx.enter_context(tc.tile_pool(name="keep", bufs=1))
+        shared = ctx.enter_context(tc.tile_pool(name="shared", bufs=1))
         late = ctx.enter_context(tc.tile_pool(name="late", bufs=2))
         psum = ctx.enter_context(tc.psum_pool(name="psum", bufs=1))
 
@@ -59,7 +59,7 @@ def tile_moe_pln_mlp_silu_kernel(
             for n, slab in enumerate(range(SLABS)[run]):
                 slab_plane[slab] = plane[:, n * H : (n + 1) * H]
         w2_plane = keep.tile([P, E * H_PASSES * N], U8, name="w2s", align_bytes=ALIGN)
-        for plane in w1_planes + [w2_plane]:
+        for plane in [w2_plane] + w1_planes:
             nc.vector.memset(plane[:].bitcast(I32), 0)
 
         result = keep.tile([P, T], F32, name="result", align_bytes=ALIGN)
@@ -75,11 +75,14 @@ def tile_moe_pln_mlp_silu_kernel(
 
         def load_x(s, u):
             rows = xT[PASS * s : PASS * (s + 1), :].rearrange("(p d) w -> p d w", d=4)
-            raw[s, u] = keep.tile([P, 2, T], F32, name=f"raw{s}{u}", align_bytes=ALIGN)
+            if (s, u) == (LAST, 0):
+                raw[s, u] = shared.tile([P, 2, T], F32, name="raw_shared", align_bytes=ALIGN, offset=0)
+            else:
+                raw[s, u] = keep.tile([P, 2, T], F32, name=f"raw{s}{u}", align_bytes=ALIGN)
             nc.sync.dma_start(out=raw[s, u][:], in_=rows[:, 2 * u : 2 * u + 2, :])
 
-        def load_scales(plane, rows):
-            for r in range(4):
+        def load_scales(plane, rows, quarters=range(4)):
+            for r in quarters:
                 nc.sync.dma_start(
                     out=plane[r:P:32, :].bitcast(I32).rearrange("q (s i) -> q s i", s=rows.shape[0]),
                     in_=rows[:, r:16:4, :].bitcast(I32).rearrange("s q i -> q s i"),
@@ -92,21 +95,22 @@ def tile_moe_pln_mlp_silu_kernel(
 
         load_x(0, 0)
         nc.sync.dma_start(offsets[:], offs)
-        for s, u in ((0, 1), (1, 0), (1, 1)):
+        w2_rows = w2_scales.rearrange("e s q i -> (e s) q i")
+        load_scales(w2_plane, w2_rows, range(2))
+        for s, u in ((0, 1), (1, 0), (1, 1), (LAST, 0)):
             load_x(s, u)
         w1_rows = w1_scales.rearrange("e s q i -> (e s) q i")
         load_scales(w1_planes[0], w1_rows[RUNS[0]])
         load_slab(0)
-        load_x(LAST, 0)
-        load_slab(K_PASSES)
-        load_scales(w2_plane, w2_scales.rearrange("e s q i -> (e s) q i"))
         load_x(LAST, 1)
         load_scales(w1_planes[1], w1_rows[RUNS[1]])
+        load_slab(K_PASSES)
         load_slab(1)
         load_scales(w1_planes[2], w1_rows[RUNS[2]])
         load_slab(LAST)
         for slab in range(K_PASSES + 1, SLABS):
             load_slab(slab)
+        load_scales(w2_plane, w2_rows, range(2, 4))
         nc.sync.dma_start(
             out=w2[:].rearrange("p e b -> p (e b)").bitcast(I32).rearrange("p (e b) -> p e b", e=E * H_PASSES),
             in_=w2_words.bitcast(I32).rearrange("e s p b -> p (e s) b"),
@@ -141,11 +145,11 @@ def tile_moe_pln_mlp_silu_kernel(
                 runs[:, u, first : first + groups * P], pairs_of[s, u].indirect(entries(group * P, groups * P))
             )
 
-        def weave(s, group, groups, pool, name, copy=nc.vector.tensor_copy, word=I32):
+        def weave(s, group, groups, copy, word, woven):
             runs, first = apart[s, group]
-            picked[s, group] = pool.tile([P, groups * P, 4], BF16, name=name, align_bytes=ALIGN)
+            picked[s, group] = woven
             copy(
-                picked[s, group][:].bitcast(word),
+                woven[:].bitcast(word),
                 runs[:, :, first : first + groups * P].bitcast(word).rearrange("p u j -> p j u"),
             )
 
@@ -191,7 +195,7 @@ def tile_moe_pln_mlp_silu_kernel(
                 nc.tensor.transpose(turned[group, g][:, run], hidden[group, g][:].bitcast(F32)[:, run], ident[:])
 
         def interleave(group, g):
-            copy = nc.vector.tensor_copy if group < PER_EXPERT else nc.scalar.copy
+            copy = nc.vector.tensor_copy if group < PER_EXPERT or (group, g) == (2, 1) else nc.scalar.copy
             values[group, g] = keep.tile([P, PASS], BF16, name=f"hb{group}_{g}", align_bytes=ALIGN)
             copy(
                 values[group, g][:].bitcast(F32).rearrange("p (r u) -> p r u", u=2),
@@ -210,7 +214,7 @@ def tile_moe_pln_mlp_silu_kernel(
                     step(group, g)
 
         def second_product(group):
-            sums[group] = bank(SUMS_BANK[group], 0, "y")
+            sums[group] = bank(group, 0, "y")
             for g in range(H_PASSES):
                 words, planes = codes[group, g]
                 row = (group // PER_EXPERT) * H_PASSES + g
@@ -224,10 +228,8 @@ def tile_moe_pln_mlp_silu_kernel(
                     stop=(g == H_PASSES - 1),
                 )
 
-        def put_back(group):
-            copy = nc.vector.tensor_copy if group == 0 else nc.scalar.copy
-            name = f"hs{group + 1}_{H_PASSES - 1}"
-            staged[group] = keep.tile([P, P], F32, name=name, align_bytes=ALIGN)
+        def put_back(group, copy):
+            staged[group] = keep.tile([P, P], F32, name=f"yt{group}", align_bytes=ALIGN)
             copy(staged[group][:], sums[group][:, 0:P])
             nc.vector.tensor_tensor(
                 result[:].indirect(entries(group * P, P)),
@@ -236,27 +238,31 @@ def tile_moe_pln_mlp_silu_kernel(
                 MULT,
             )
 
-        experts = [(e * PER_EXPERT, PER_EXPERT) for e in range(E)]
         for s in range(LAST):
-            for group, groups in experts:
-                runs_tile(s, group, groups, keep, f"xa{s}{group}")
+            for group in range(0, GROUPS, PER_EXPERT):
+                runs_tile(s, group, PER_EXPERT, keep, f"xa{s}{group}")
             for u in range(2):
                 round_pair(s, u)
-                for group, groups in experts:
-                    gather(s, u, group, groups)
-            weave(s, 0, PER_EXPERT, keep, f"xg{s}")
-            quantise(s, 0, PER_EXPERT)
-        weave(0, PER_EXPERT, PER_EXPERT, keep, "raw11", nc.scalar.copy, U32)
-        quantise(0, PER_EXPERT, PER_EXPERT)
+                for group in range(0, GROUPS, PER_EXPERT):
+                    gather(s, u, group, PER_EXPERT)
+            if s == 0:
+                woven = keep.tile([P, C, 4], BF16, name="xg0", align_bytes=ALIGN)
+                weave(0, 0, PER_EXPERT, nc.vector.tensor_copy, I32, woven)
+                quantise(0, 0, PER_EXPERT)
         runs_tile(LAST, 0, PER_EXPERT, keep, "xa_last")
         round_pair(LAST, 0)
         gather(LAST, 0, 0, PER_EXPERT)
+        for n, (s, group) in enumerate(((0, PER_EXPERT), (1, 0))):
+            woven = shared.tile([P, C, 4], BF16, name=f"xg_shared{n}", align_bytes=ALIGN, offset=n * C * 8)
+            weave(s, group, PER_EXPERT, nc.scalar.copy, U32, woven)
+            quantise(s, group, PER_EXPERT)
         round_pair(LAST, 1)
-        weave(1, PER_EXPERT, PER_EXPERT, keep, "raw21", nc.scalar.copy, U32)
+        woven = keep.tile([P, C, 4], BF16, name=f"raw{LAST}1", align_bytes=ALIGN)
+        weave(1, PER_EXPERT, PER_EXPERT, nc.scalar.copy, U32, woven)
         for group in range(PER_EXPERT):
             gather(LAST, 1, group, 1)
         for group in range(PER_EXPERT):
-            weave(LAST, group, 1, late, "late", nc.scalar.copy, U32)
+            weave(LAST, group, 1, nc.scalar.copy, U32, late.tile([P, P, 4], BF16, name="late", align_bytes=ALIGN))
         for group in range(PER_EXPERT):
             quantise(LAST, group, 1)
         quantise(1, PER_EXPERT, PER_EXPERT)
@@ -264,7 +270,8 @@ def tile_moe_pln_mlp_silu_kernel(
             runs_tile(LAST, group, 1, late, "late")
             for u in range(2):
                 gather(LAST, u, group, 1)
-            weave(LAST, group, 1, keep, f"xg_last{group}")
+            woven = keep.tile([P, P, 4], BF16, name=f"xg_last{group}", align_bytes=ALIGN)
+            weave(LAST, group, 1, nc.vector.tensor_copy, I32, woven)
             quantise(LAST, group, 1)
 
         for group in range(GROUPS):
@@ -282,20 +289,21 @@ def tile_moe_pln_mlp_silu_kernel(
             activate(2, g)
         hand_over(1)
         second_product(0)
-        put_back(0)
-        for s in range(1, K_PASSES):
-            first_product(3, s, (0,))
-        activate(3, 0)
+        put_back(0, nc.vector.tensor_copy)
+        for g in range(H_PASSES):
+            for s in range(1, K_PASSES):
+                first_product(3, s, (g,))
+            activate(3, g)
         hand_over(2)
+        turn(3, 0)
         second_product(1)
-        put_back(1)
-        for s in range(1, K_PASSES):
-            first_product(3, s, (1,))
-        activate(3, 1)
-        hand_over(3)
-        second_product(2)
-        put_back(2)
-        second_product(3)
-        put_back(3)
+        turn(3, 1)
+        for step in (interleave, quantise_hidden):
+            for g in range(H_PASSES):
+                step(3, g)
+        put_back(1, nc.scalar.copy)
+        for group in range(PER_EXPERT, GROUPS):
+            second_product(group)
+            put_back(group, nc.scalar.copy)
 
         nc.sync.dma_start(out=out, in_=result[:])

from contextlib import ExitStack

import concourse.mybir as mybir
from concourse.masks import make_identity

F32 = mybir.dt.float32
BF16 = mybir.dt.bfloat16
I32 = mybir.dt.int32
U32 = mybir.dt.uint32
U16 = mybir.dt.uint16
U8 = mybir.dt.uint8
FP8X4 = mybir.dt.float8_e4m3fn_x4
FP4X4 = mybir.dt.float4_e2m1fn_x4
COPY = mybir.ActivationFunctionType.Copy
SILU = mybir.ActivationFunctionType.Silu
MULT = mybir.AluOpType.mult

P = 128
K, T, E, C, H, N = 1536, 640, 2, 256, 1024, 128
PASS = 512
K_PASSES = K // PASS
H_PASSES = H // PASS
LAST = K_PASSES - 1
GROUPS = E * C // P
PER_EXPERT = C // P
SLABS = E * K_PASSES
LIST_ROWS = 16
ALIGN = 256
FLOPS = 2 * E * C * (K * H + H * N)

SCALAR_TOKENS = {(0, 0): 224, (0, 1): 448, (LAST, 1): 384}
RUNS = (slice(0, SLABS, K_PASSES), slice(1, K_PASSES), slice(K_PASSES + 1, SLABS))
RUN = 2


def tile_moe_pln_mlp_silu_kernel(
    tc, xT, w1_words, w1_scales, w2_words, w2_scales, gate, offs, out
):
    nc = tc.nc
    with ExitStack() as ctx:
        lists = ctx.enter_context(tc.tile_pool(name="lists", bufs=1))
        keep = ctx.enter_context(tc.tile_pool(name="keep", bufs=1))
        shared = ctx.enter_context(tc.tile_pool(name="shared", bufs=1))
        late = ctx.enter_context(tc.tile_pool(name="late", bufs=2))
        psum = ctx.enter_context(tc.psum_pool(name="psum", bufs=1))

        offsets = lists.tile([P, E * C // LIST_ROWS], U16, name="offsets")

        def entries(slot, count):
            return offsets[:, slot // LIST_ROWS : (slot + count) // LIST_ROWS]

        warm = keep.tile([P, 2], F32, name="warm", align_bytes=ALIGN)
        nc.vector.memset(warm[:, 0:1], 0.0)
        nc.scalar.activation(warm[:, 1:2], warm[:, 0:1], SILU)

        w1_planes = [keep.tile([P, RUN * H], U8, name=f"w1s{r}", align_bytes=ALIGN) for r in range(len(RUNS))]
        slab_plane = {}
        for plane, run in zip(w1_planes, RUNS):
            for n, slab in enumerate(range(SLABS)[run]):
                slab_plane[slab] = plane[:, n * H : (n + 1) * H]
        w2_plane = keep.tile([P, E * H_PASSES * N], U8, name="w2s", align_bytes=ALIGN)
        for plane in [w2_plane] + w1_planes:
            nc.vector.memset(plane[:].bitcast(I32), 0)

        result = keep.tile([P, T], F32, name="result", align_bytes=ALIGN)
        nc.vector.memset(result[:], 0.0)

        ident = keep.tile([P, P], F32, name="ident", align_bytes=ALIGN)
        make_identity(nc, ident[:])

        raw = {}
        w1 = {}
        w2 = keep.tile([P, E * H_PASSES, 2 * N], U8, name="w2", align_bytes=ALIGN)
        gates = keep.tile([P, E * C], F32, name="gates", align_bytes=ALIGN)

        def load_x(s, u):
            rows = xT[PASS * s : PASS * (s + 1), :].rearrange("(p d) w -> p d w", d=4)
            if (s, u) == (LAST, 0):
                raw[s, u] = shared.tile([P, 2, T], F32, name="raw_shared", align_bytes=ALIGN, offset=0)
            else:
                raw[s, u] = keep.tile([P, 2, T], F32, name=f"raw{s}{u}", align_bytes=ALIGN)
            nc.sync.dma_start(out=raw[s, u][:], in_=rows[:, 2 * u : 2 * u + 2, :])

        def load_scales(plane, rows, quarters=range(4)):
            for r in quarters:
                nc.sync.dma_start(
                    out=plane[r:P:32, :].bitcast(I32).rearrange("q (s i) -> q s i", s=rows.shape[0]),
                    in_=rows[:, r:16:4, :].bitcast(I32).rearrange("s q i -> q s i"),
                )

        def load_slab(slab):
            words = keep.tile([P, 2 * H], U8, name=f"w1_{slab}", align_bytes=ALIGN)
            nc.sync.dma_start(out=words[:].bitcast(I32), in_=w1_words[slab // K_PASSES, slab % K_PASSES].bitcast(I32))
            w1[slab] = words

        load_x(0, 0)
        nc.sync.dma_start(offsets[:], offs)
        w2_rows = w2_scales.rearrange("e s q i -> (e s) q i")
        load_scales(w2_plane, w2_rows, range(2))
        for s, u in ((0, 1), (1, 0), (1, 1), (LAST, 0)):
            load_x(s, u)
        w1_rows = w1_scales.rearrange("e s q i -> (e s) q i")
        load_scales(w1_planes[0], w1_rows[RUNS[0]])
        load_slab(0)
        load_x(LAST, 1)
        load_scales(w1_planes[1], w1_rows[RUNS[1]])
        load_slab(K_PASSES)
        load_slab(1)
        load_scales(w1_planes[2], w1_rows[RUNS[2]])
        load_slab(LAST)
        for slab in range(K_PASSES + 1, SLABS):
            load_slab(slab)
        load_scales(w2_plane, w2_rows, range(2, 4))
        nc.sync.dma_start(
            out=w2[:].rearrange("p e b -> p (e b)").bitcast(I32).rearrange("p (e b) -> p e b", e=E * H_PASSES),
            in_=w2_words.bitcast(I32).rearrange("e s p b -> p (e s) b"),
        )
        nc.sync.dma_start(out=gates[:], in_=gate)

        def bank(group, g, name):
            number = H_PASSES * group + g
            return psum.tile([P, PASS], F32, name=f"{name}{number}", tag=f"bank{number}")

        acc = {(group, g): bank(group, g, "acc") for group in range(GROUPS) for g in range(H_PASSES)}

        pairs_of, apart, picked, slot_words, slot_planes = {}, {}, {}, {}, {}

        def round_pair(s, u):
            rounded = keep.tile([P, T, 2], BF16, name=f"xb{s}{u}", align_bytes=ALIGN)
            share = SCALAR_TOKENS.get((s, u), T)
            src = raw[s, u][:].rearrange("p d w -> p w d")
            nc.scalar.activation(rounded[:, 0:share, :], src[:, 0:share, :], COPY)
            if share < T:
                nc.vector.tensor_copy(rounded[:, share:T, :], src[:, share:T, :])
            pairs_of[s, u] = rounded[:].rearrange("p w d -> p (w d)").bitcast(U32)

        def runs_tile(s, group, groups, pool, name):
            runs = pool.tile([P, 2, groups * P], U32, name=name, align_bytes=ALIGN)
            for c in range(groups):
                apart[s, group + c] = (runs, c * P)

        def gather(s, u, group, groups):
            runs, first = apart[s, group]
            nc.vector.tensor_copy(
                runs[:, u, first : first + groups * P], pairs_of[s, u].indirect(entries(group * P, groups * P))
            )

        def weave(s, group, groups, copy, word, woven):
            runs, first = apart[s, group]
            picked[s, group] = woven
            copy(
                woven[:].bitcast(word),
                runs[:, :, first : first + groups * P].bitcast(word).rearrange("p u j -> p j u"),
            )

        def quantise(s, group, groups):
            words = keep.tile([P, groups * P], U32, name=f"xw{s}{group}", align_bytes=ALIGN)
            planes = keep.tile([P, groups * P], U8, name=f"xs{s}{group}", align_bytes=ALIGN)
            nc.vector.quantize_mx(
                out=words[:].bitcast(FP8X4),
                scales=planes[:],
                in_=picked[s, group][:].rearrange("p j d -> p (j d)"),
            )
            for c in range(groups):
                slot_words[s, group + c] = words[:, c * P : (c + 1) * P]
                slot_planes[s, group + c] = planes[:, c * P : (c + 1) * P]

        hidden, turned, values, codes, sums, staged = {}, {}, {}, {}, {}, {}

        def first_product(group, s, halves=range(H_PASSES)):
            slab = (group // PER_EXPERT) * K_PASSES + s
            for g in halves:
                nc.tensor.matmul_mx(
                    out=acc[group, g][:],
                    lhsT=slot_words[s, group].bitcast(FP8X4),
                    lhsT_scale=slot_planes[s, group],
                    rhs=w1[slab][:, 2 * g * PASS : 2 * (g + 1) * PASS].bitcast(FP4X4),
                    rhs_scale=slab_plane[slab][:, g * PASS : (g + 1) * PASS],
                    start=(s == 0),
                    stop=(s == LAST),
                )

        def activate(group, g):
            hidden[group, g] = keep.tile([P, PASS], BF16, name=f"hs{group}_{g}", align_bytes=ALIGN)
            nc.scalar.activation(
                hidden[group, g][:].rearrange("p (u m d) -> p u m d", u=2, d=2),
                acc[group, g][:].rearrange("p (m u d) -> p u m d", u=2, d=2),
                SILU,
            )

        def turn(group, g):
            turned[group, g] = bank(group, g, "tp")[:, 0 : 2 * P]
            for u in range(2):
                run = slice(u * P, (u + 1) * P)
                nc.tensor.transpose(turned[group, g][:, run], hidden[group, g][:].bitcast(F32)[:, run], ident[:])

        def interleave(group, g):
            copy = nc.vector.tensor_copy if group < PER_EXPERT or (group, g) == (2, 1) else nc.scalar.copy
            values[group, g] = keep.tile([P, PASS], BF16, name=f"hb{group}_{g}", align_bytes=ALIGN)
            copy(
                values[group, g][:].bitcast(F32).rearrange("p (r u) -> p r u", u=2),
                turned[group, g].rearrange("p (u r) -> p r u", u=2),
            )

        def quantise_hidden(group, g):
            words = keep.tile([P, P], U32, name=f"hw{group}_{g}", align_bytes=ALIGN)
            planes = keep.tile([P, P], U8, name=f"hc{group}_{g}", align_bytes=ALIGN)
            nc.vector.quantize_mx(out=words[:].bitcast(FP8X4), scales=planes[:], in_=values[group, g][:])
            codes[group, g] = (words, planes)

        def hand_over(group):
            for step in (turn, interleave, quantise_hidden):
                for g in range(H_PASSES):
                    step(group, g)

        def second_product(group):
            sums[group] = bank(group, 0, "y")
            for g in range(H_PASSES):
                words, planes = codes[group, g]
                row = (group // PER_EXPERT) * H_PASSES + g
                nc.tensor.matmul_mx(
                    out=sums[group][:, 0:P],
                    lhsT=w2[:, row, :].bitcast(FP4X4),
                    lhsT_scale=w2_plane[:, row * N : (row + 1) * N],
                    rhs=words[:].bitcast(FP8X4),
                    rhs_scale=planes[:],
                    start=(g == 0),
                    stop=(g == H_PASSES - 1),
                )

        def put_back(group, copy):
            staged[group] = keep.tile([P, P], F32, name=f"yt{group}", align_bytes=ALIGN)
            copy(staged[group][:], sums[group][:, 0:P])
            nc.vector.tensor_tensor(
                result[:].indirect(entries(group * P, P)),
                staged[group][:],
                gates[:, group * P : (group + 1) * P],
                MULT,
            )

        for s in range(LAST):
            for group in range(0, GROUPS, PER_EXPERT):
                runs_tile(s, group, PER_EXPERT, keep, f"xa{s}{group}")
            for u in range(2):
                round_pair(s, u)
                for group in range(0, GROUPS, PER_EXPERT):
                    gather(s, u, group, PER_EXPERT)
            if s == 0:
                woven = keep.tile([P, C, 4], BF16, name="xg0", align_bytes=ALIGN)
                weave(0, 0, PER_EXPERT, nc.vector.tensor_copy, I32, woven)
                quantise(0, 0, PER_EXPERT)
        runs_tile(LAST, 0, PER_EXPERT, keep, "xa_last")
        round_pair(LAST, 0)
        gather(LAST, 0, 0, PER_EXPERT)
        for n, (s, group) in enumerate(((0, PER_EXPERT), (1, 0))):
            woven = shared.tile([P, C, 4], BF16, name=f"xg_shared{n}", align_bytes=ALIGN, offset=n * C * 8)
            weave(s, group, PER_EXPERT, nc.scalar.copy, U32, woven)
            quantise(s, group, PER_EXPERT)
        round_pair(LAST, 1)
        woven = keep.tile([P, C, 4], BF16, name=f"raw{LAST}1", align_bytes=ALIGN)
        weave(1, PER_EXPERT, PER_EXPERT, nc.scalar.copy, U32, woven)
        for group in range(PER_EXPERT):
            gather(LAST, 1, group, 1)
        for group in range(PER_EXPERT):
            weave(LAST, group, 1, nc.scalar.copy, U32, late.tile([P, P, 4], BF16, name="late", align_bytes=ALIGN))
        for group in range(PER_EXPERT):
            quantise(LAST, group, 1)
        quantise(1, PER_EXPERT, PER_EXPERT)
        for group in range(PER_EXPERT, GROUPS):
            runs_tile(LAST, group, 1, late, "late")
            for u in range(2):
                gather(LAST, u, group, 1)
            woven = keep.tile([P, P, 4], BF16, name=f"xg_last{group}", align_bytes=ALIGN)
            weave(LAST, group, 1, nc.vector.tensor_copy, I32, woven)
            quantise(LAST, group, 1)

        for group in range(GROUPS):
            first_product(group, 0)
        for group in range(PER_EXPERT):
            first_product(group, 1)
        for group in range(PER_EXPERT):
            first_product(group, LAST)
            for g in range(H_PASSES):
                activate(group, g)
        first_product(2, 1)
        hand_over(0)
        first_product(2, LAST)
        for g in range(H_PASSES):
            activate(2, g)
        hand_over(1)
        second_product(0)
        put_back(0, nc.vector.tensor_copy)
        for g in range(H_PASSES):
            for s in range(1, K_PASSES):
                first_product(3, s, (g,))
            activate(3, g)
        hand_over(2)
        turn(3, 0)
        second_product(1)
        turn(3, 1)
        for step in (interleave, quantise_hidden):
            for g in range(H_PASSES):
                step(3, g)
        put_back(1, nc.scalar.copy)
        for group in range(PER_EXPERT, GROUPS):
            second_product(group)
            put_back(group, nc.scalar.copy)

        nc.sync.dma_start(out=out, in_=result[:])
